import numpy as np
import ml_dtypes


def mxq(x, axis, fmt="e4m3"):
    dtype, down = {"e4m3": (ml_dtypes.float8_e4m3fn, 7), "e5m2": (ml_dtypes.float8_e5m2, 14)}[fmt]
    v = np.moveaxis(np.asarray(x, np.float32).astype(ml_dtypes.bfloat16).astype(np.float64), axis, -1)
    blocks = v.reshape(v.shape[:-1] + (-1, 32))
    amax = np.abs(blocks).max(-1, keepdims=True)
    byte = np.maximum(np.where(amax > 0, np.frexp(amax)[1] - 1 + 127, 0) - down, 1)
    scale = np.exp2(byte - 127.0)
    codes = (blocks / scale).astype(np.float32).astype(dtype).astype(np.float64)
    return np.moveaxis((codes * scale).reshape(v.shape), -1, axis)


WIDE = False


def mx_kscale(k):
    if not WIDE:
        return np.ones(k)
    levels = np.array([10, -10, 5, -5, 0])
    if k % 512:
        return np.exp2(np.random.permutation(np.resize(levels, k // 32))).repeat(32)
    a = np.empty((k // 512, 16))
    for p in range(k // 512):
        a[p, :8] = np.random.permutation(np.resize(levels, 8))
        for g in range(8):
            far = levels[np.abs(levels - a[p, g]) >= 10]
            a[p, g + 8] = far[np.random.randint(len(far))]
    return np.exp2(a.ravel()).repeat(32)


def f64(x):
    return np.asarray(x).astype(np.float64)


def striped(idx):
    return np.tile(idx.reshape(-1, 16).T, (8, 1)).astype(np.uint16)


def unstriped(offs):
    return offs[:16].T.reshape(-1).astype(np.int64)


def striped8(idx):
    return np.concatenate([x.reshape(-1, 16).T for x in idx]).astype(np.uint16)


def runs(offs, k):
    lists = np.stack([offs[16 * r : 16 * r + 16].T.reshape(-1) for r in range(8)]).astype(np.int64)
    return lists[np.arange(k) % 512 // 64]


def pack_weight(w):
    k, n = w.shape
    w = f64(np.asarray(w, np.float32).astype(ml_dtypes.bfloat16)).reshape(k // 32, 32, n)
    amax = np.abs(w).max(1)
    byte = np.clip(np.where(amax > 0, np.frexp(amax)[1] - 1 + 127 - 7, 1), 1, 254)
    scaled = (w * np.exp2(127.0 - byte)[:, None, :]).reshape(k, n).astype(np.float32)
    words = np.ascontiguousarray(scaled.reshape(k // 512, 128, 4, n).transpose(0, 1, 3, 2)).astype(ml_dtypes.float8_e4m3fn).view(np.uint8)
    return words, np.ascontiguousarray(byte.astype(np.uint8).reshape(k // 512, 16, n))


def unpack_weight(words, scales):
    g, p, n, _ = words.shape
    vals = np.ascontiguousarray(words).view(ml_dtypes.float8_e4m3fn).astype(np.float64) * np.repeat(np.exp2(scales.astype(np.float64) - 127.0), 8, axis=1)[..., None]
    return vals.transpose(0, 1, 3, 2).reshape(g * 512, n)


K, T, S, H, C = 512, 2048, 512, 512, 512


def setup_inputs():
    n = np.random.standard_normal
    s = mx_kscale(K)[:, None]
    packed_xT = pack_weight(n((K, T)) * s)
    return {
        "x_words": packed_xT[0],
        "x_scales": packed_xT[1],
        "w1": (n((K, H)) / np.sqrt(K) / s).astype(np.float32),
        "gs": (np.random.uniform(0.5, 1.5, (K, 1)) / s).astype(np.float32),
        "offs": striped(np.random.permutation(T)[:S]),
        "n1": striped8(np.stack([np.random.permutation(S) for _ in range(8)])),
        "n2": striped8(np.stack([np.random.permutation(S) for _ in range(8)])),
        "ca": striped(np.random.permutation(T)[:C]),
        "cb": striped(np.random.permutation(T)[:C]),
        "cd": striped(np.random.permutation(T)[:C]),
        "n3": striped8(np.stack([np.random.permutation(S) for _ in range(8)])),
        "n4": striped8(np.stack([np.random.permutation(S) for _ in range(8)])),
        "n5": striped8(np.stack([np.random.permutation(S) for _ in range(8)])),
        "n6": striped8(np.stack([np.random.permutation(S) for _ in range(8)])),
        "n7": striped8(np.stack([np.random.permutation(S) for _ in range(8)])),
    }


def reference(x_words, x_scales, w1, gs, offs, n1, n2, ca, cb, cd, n3, n4, n5, n6, n7):
    x_cb = unpack_weight(x_words, x_scales)[:, unstriped(cb)]
    xq = unpack_weight(x_words, x_scales)[:, unstriped(offs)]
    y = mxq(f64(w1), 0, "e4m3").T @ xq
    pa = y[np.arange(H)[:, None], runs(n1, H)]
    pb = y[np.arange(H)[:, None], runs(n2, H)]
    z = f64(gs) * (np.maximum(np.minimum(y, pa), np.minimum(np.maximum(y, pa), pb)))
    zq = mxq(z, 0, "e4m3")
    b = 0.0625 * (x_cb.T @ zq)
    x_ca = unpack_weight(x_words, x_scales)[:, unstriped(ca)]
    a = 0.0625 * (x_ca.T @ zq)
    m1 = b * (a[np.arange(C)[:, None], runs(n3, C)] - a) + 0.5 * ((b[np.arange(C)[:, None], runs(n5, C)]) * (a[np.arange(C)[:, None], runs(n4, C)] - a))
    x_cd = unpack_weight(x_words, x_scales)[:, unstriped(cd)]
    q = 0.0625 * (x_cd.T @ zq)
    return np.maximum(m1, q[np.arange(C)[:, None], runs(n7, C)]) - (np.minimum(m1[np.arange(C)[:, None], runs(n6, C)], q))

@@ -1,0 +1,250 @@
+from contextlib import ExitStack
+
+import concourse.mybir as mybir
+
+K, T, S, H, C = 512, 2048, 512, 512, 512
+FLOPS = 4 * 2 * 512 * 512 * 512
+
+F32 = mybir.dt.float32
+BF16 = mybir.dt.bfloat16
+I32 = mybir.dt.int32
+U32 = mybir.dt.uint32
+U16 = mybir.dt.uint16
+U8 = mybir.dt.uint8
+FP8X4 = mybir.dt.float8_e4m3fn_x4
+ALU = mybir.AluOpType
+COPY = mybir.ActivationFunctionType.Copy
+
+P = 128
+PACK = 4
+TILES = 4
+HALF = S // 2
+SCORE_SCALE = 0.0625
+VECTOR_PB = [(1, 0), (3, 0)]
+VECTOR_A3 = [(1, 1)]
+VECTOR_M6 = [(3, 0)]
+
+
+def tile_picked_tricdflowbmaxbmed_none_p_kernel(
+    tc, x_words, x_scales, w1, gs, offs, n1, n2, ca, cb, cd, n3, n4, n5, n6, n7, out
+):
+    nc = tc.nc
+    with ExitStack() as ctx:
+        lists = ctx.enter_context(tc.tile_pool(name="lists", bufs=1))
+        keep = ctx.enter_context(tc.tile_pool(name="keep", bufs=1))
+        work = ctx.enter_context(tc.tile_pool(name="work", bufs=2))
+        psum = ctx.enter_context(tc.psum_pool(name="psum", bufs=8))
+
+        def load_list(src, name):
+            dst = lists.tile([P, S // 16], U16, name=name)
+            nc.sync.dma_start(dst[:], src)
+            return dst
+
+        def cols(h):
+            return slice(h * HALF, (h + 1) * HALF)
+
+        def half_of(lst, h):
+            return lst[:, h * HALF // 16 : (h + 1) * HALF // 16]
+
+        l_offs = load_list(offs, "l_offs")
+        l_ca = load_list(ca, "l_ca")
+        l_cb = load_list(cb, "l_cb")
+        table_scales = keep.tile([P, T], U8, name="table_scales", align_bytes=64)
+        nc.vector.memset(table_scales[:].bitcast(I32), 0)
+        for quad in range(4):
+            nc.sync.dma_start(
+                table_scales[32 * quad : 32 * quad + 4, :].bitcast(I32),
+                x_scales[0, 4 * quad : 4 * quad + 4, :].bitcast(I32),
+            )
+        w_raw = keep.tile([P, PACK, H], F32, name="w_raw")
+        nc.sync.dma_start(w_raw[:], w1.rearrange("(p j) c -> p j c", j=PACK))
+        table_words = keep.tile([P, T], U32, name="table_words", align_bytes=64)
+        nc.sync.dma_start(
+            table_words[:].bitcast(I32), x_words[0].rearrange("p n r -> p (n r)").bitcast(I32)
+        )
+        gain = keep.tile([P, TILES], F32, name="gain")
+        nc.sync.dma_start(gain[:], gs.rearrange("(p t) o -> p (t o)", t=TILES))
+        l_n1 = load_list(n1, "l_n1")
+        l_n2 = load_list(n2, "l_n2")
+        l_cd = load_list(cd, "l_cd")
+        l_n3 = load_list(n3, "l_n3")
+        l_n4 = load_list(n4, "l_n4")
+        l_n5 = load_list(n5, "l_n5")
+        l_n7 = load_list(n7, "l_n7")
+        l_n6 = load_list(n6, "l_n6")
+
+        def pick_scales(lst, name, tag=None):
+            dst = keep.tile([P, S], U8, name=name, tag=tag or name, align_bytes=64)
+            nc.vector.tensor_copy(dst[:], table_scales[:].indirect(lst[:]))
+            return dst
+
+        def pick_dealt_scales(lst, name, tag=None):
+            picked = pick_scales(lst, name + "_picked", tag)
+            dst = keep.tile([P, S], U8, name=name, align_bytes=64)
+            nc.vector.tensor_copy(
+                dst[:].bitcast(I32).rearrange("p (t a) -> p t a", t=TILES),
+                picked[:].bitcast(I32).rearrange("p (a t) -> p t a", t=TILES),
+            )
+            return dst
+
+        def pick_dealt_words(lst, name, tag):
+            dst = keep.tile([P, S], U32, name=name, tag=tag, align_bytes=64)
+            nc.vector.tensor_copy(
+                dst[:].rearrange("p (t a v) -> p a t v", t=TILES, v=4), table_words[:].indirect(lst[:])
+            )
+            return dst
+
+        token_scales = pick_scales(l_offs, "token_scales")
+        a_scales = pick_dealt_scales(l_ca, "a_scales")
+
+        b_scales = pick_dealt_scales(l_cb, "b_scales")
+
+        w_codes = keep.tile([P, H], U32, name="w_codes", align_bytes=64)
+        w_scales = keep.tile([P, H], U8, name="w_scales", align_bytes=64)
+        token_words = keep.tile([P, S], U32, name="token_words", align_bytes=64)
+
+        def quantize_weights(pair):
+            w_bf = keep.tile([P, 2, P, PACK], BF16, name="w_bf", tag=f"w_pair{pair}", align_bytes=64)
+            nc.scalar.copy(
+                w_bf[:].rearrange("p t m j -> p m j t"),
+                w_raw[:].rearrange("p j (m t) -> p m j t", t=TILES)[:, :, :, 2 * pair : 2 * pair + 2],
+            )
+            nc.vector.quantize_mx(
+                out=w_codes[:, cols(pair)].bitcast(FP8X4),
+                scales=w_scales[:, cols(pair)],
+                in_=w_bf[:].rearrange("p t m j -> p (t m j)"),
+            )
+
+        quantize_weights(0)
+        for h in range(2):
+            nc.vector.tensor_copy(token_words[:, cols(h)], table_words[:].indirect(half_of(l_offs, h)))
+        quantize_weights(1)
+
+        def product(width, lhs_words, lhs_scales, t, rhs_words, rhs_scales):
+            acc = psum.tile([P, width], F32, name="acc")
+            rows = slice(t * P, (t + 1) * P)
+            nc.tensor.matmul_mx(
+                out=acc[:],
+                lhsT=lhs_words[:, rows].bitcast(FP8X4),
+                lhsT_scale=lhs_scales[:, rows],
+                rhs=rhs_words.bitcast(FP8X4),
+                rhs_scale=rhs_scales,
+                start=True,
+                stop=True,
+            )
+            return acc
+
+        a_words = pick_dealt_words(l_ca, "a_words", "w_pair0")
+        b_words = pick_dealt_words(l_cb, "b_words", "w_pair1")
+
+        y = [keep.tile([P, S], F32, name=f"y{t}") for t in range(TILES)]
+        a = [keep.tile([P, S], F32, name=f"a{t}") for t in range(TILES)]
+        b = [keep.tile([P, S], F32, name=f"b{t}") for t in range(TILES)]
+        q = {}
+        z_codes = keep.tile([P, S], U32, name="z_codes", align_bytes=64)
+        z_scales = keep.tile([P, S], U8, name="z_scales", align_bytes=64)
+
+        def median_half(h):
+            low = work.tile([P, TILES, HALF], F32, name="low")
+            mid = work.tile([P, TILES, HALF], F32, name="mid")
+            for t in range(TILES):
+                if h == 0 and t == 0:
+                    for g in range(2):
+                        acc = product(HALF, w_codes, w_scales, t, token_words[:, cols(g)], token_scales[:, cols(g)])
+                        nc.scalar.activation(y[t][:, cols(g)], acc[:], COPY, scale=gain[:, t : t + 1])
+                elif h == 0:
+                    acc = product(S, w_codes, w_scales, t, token_words[:], token_scales[:])
+                    nc.scalar.activation(y[t][:], acc[:], COPY, scale=gain[:, t : t + 1])
+                pa = work.tile([P, HALF], F32, name="pa", bufs=4)
+                pb = work.tile([P, HALF], F32, name="pb", bufs=4)
+                high = work.tile([P, HALF], F32, name="high")
+                nc.scalar.activation(pa[:], y[t][:].indirect(half_of(l_n1, h)), COPY)
+                if (t, h) in VECTOR_PB:
+                    nc.vector.tensor_copy(pb[:], y[t][:].indirect(half_of(l_n2, h)))
+                else:
+                    nc.scalar.activation(pb[:], y[t][:].indirect(half_of(l_n2, h)), COPY)
+                nc.vector.tensor_tensor(high[:], y[t][:, cols(h)], pa[:], ALU.max)
+                nc.vector.tensor_tensor(low[:, t, :], y[t][:, cols(h)], pa[:], ALU.min)
+                nc.vector.tensor_tensor(mid[:, t, :], high[:], pb[:], ALU.min)
+            z = keep.tile([P, HALF * PACK], BF16, name="z", tag=f"z{h}", align_bytes=64)
+            nc.vector.tensor_tensor(
+                z[:].rearrange("p (c i t) -> p c t i", i=2, t=PACK),
+                low[:].rearrange("p t (c i) -> p c t i", i=2),
+                mid[:].rearrange("p t (c i) -> p c t i", i=2),
+                ALU.max,
+            )
+            nc.vector.quantize_mx(out=z_codes[:, cols(h)].bitcast(FP8X4), scales=z_scales[:, cols(h)], in_=z[:])
+
+        def score(dst, words, scales, t, h):
+            acc = product(HALF, words, scales, t, z_codes[:, cols(h)], z_scales[:, cols(h)])
+            nc.scalar.activation(dst[t][:, cols(h)], acc[:], COPY, scale=SCORE_SCALE)
+
+        median_half(0)
+        median_half(1)
+        q_scales = pick_dealt_scales(l_cd, "q_scales", "z1")
+        q_words = pick_dealt_words(l_cd, "q_words", "z1")
+        for t in range(TILES):
+            score(a, a_words, a_scales, t, 0)
+            score(b, b_words, b_scales, t, 0)
+
+        out_rows = out.rearrange("(a t v) c -> t a v c", t=TILES, v=4)
+        m1 = {}
+        upper = [keep.tile([P, S], F32, name=f"upper{t}") for t in range(TILES)]
+
+        def flows(t):
+            score(a, a_words, a_scales, t, 1)
+            score(b, b_words, b_scales, t, 1)
+            a3 = work.tile([P, S], F32, name="a3")
+            a4 = work.tile([P, S], F32, name="a4", bufs=1)
+            d3 = work.tile([P, S], F32, name="d3")
+            d4 = work.tile([P, S], F32, name="d4")
+            e3 = work.tile([P, S], F32, name="e3")
+            e4 = work.tile([P, S], F32, name="e4")
+            q7 = work.tile([P, S], F32, name="q7")
+            for h in range(2):
+                nc.scalar.activation(a4[:, cols(h)], a[t][:].indirect(half_of(l_n4, h)), COPY)
+            for h in range(2):
+                fetch(a3, a[t], l_n3, h, (t, h) in VECTOR_A3)
+            if t > 0:
+                fetch_m6(t - 1)
+            q[t] = keep.tile([P, S], F32, name=f"q{t}", tag=f"chain{t}")
+            for h in range(2):
+                score(q, q_words, q_scales, t, h)
+            for h in range(2):
+                nc.scalar.activation(q7[:, cols(h)], q[t][:].indirect(half_of(l_n7, h)), COPY)
+            nc.vector.tensor_tensor(d4[:], a4[:], a[t][:], ALU.subtract)
+            for h in range(2):
+                nc.vector.tensor_tensor(e4[:, cols(h)], b[t][:].indirect(half_of(l_n5, h)), d4[:, cols(h)], ALU.mult)
+            nc.vector.tensor_tensor(d3[:], a3[:], a[t][:], ALU.subtract)
+            if t > 0:
+                finish(t - 1, [slice(0, S)])
+            nc.vector.tensor_tensor(e3[:], d3[:], b[t][:], ALU.mult)
+            m1[t] = keep.tile([P, S], F32, name=f"m1_{t}", tag=f"chain{t + 1}")
+            nc.vector.scalar_tensor_tensor(m1[t][:], e4[:], 0.5, e3[:], ALU.mult, ALU.add)
+            nc.vector.tensor_tensor(upper[t][:], m1[t][:], q7[:], ALU.max)
+
+        def fetch(dst, window, lst, h, on_vector):
+            if on_vector:
+                nc.vector.tensor_copy(dst[:, cols(h)], window[:].indirect(half_of(lst, h)))
+            else:
+                nc.scalar.activation(dst[:, cols(h)], window[:].indirect(half_of(lst, h)), COPY)
+
+        def fetch_m6(t):
+            m6[t] = work.tile([P, S], F32, name="m6")
+            for h in range(2):
+                fetch(m6[t], m1[t], l_n6, h, (t, h) in VECTOR_M6)
+
+        def finish(t, pieces):
+            lower = work.tile([P, S], F32, name="lower")
+            res = work.tile([P, S], F32, name="res")
+            for piece in pieces:
+                nc.vector.tensor_tensor(lower[:, piece], m6[t][:, piece], q[t][:, piece], ALU.min)
+            for piece in pieces:
+                nc.vector.tensor_tensor(res[:, piece], upper[t][:, piece], lower[:, piece], ALU.subtract)
+                nc.sync.dma_start(out_rows[t][:, :, piece], res[:, piece])
+
+        m6 = {}
+        for t in range(TILES):
+            flows(t)
+        fetch_m6(TILES - 1)
+        finish(TILES - 1, [cols(0), cols(1)])

@@ -20,9 +20,12 @@ PACK = 4
 TILES = 4
 HALF = S // 2
 SCORE_SCALE = 0.0625
-VECTOR_PB = [(1, 0), (3, 0)]
-VECTOR_A3 = [(1, 1)]
-VECTOR_M6 = [(3, 0)]
+GROUP = 2
+Z_PIECES = 2
+VECTOR_PB = [(0, 0), (1, 0), (2, 0), (3, 0)]
+VECTOR_A3 = []
+VECTOR_M6 = [(0, 0)]
+SCALAR_B5 = [(3, 1)]
 
 
 def tile_picked_tricdflowbmaxbmed_none_p_kernel(
@@ -32,6 +35,7 @@ def tile_picked_tricdflowbmaxbmed_none_p_kernel(
     with ExitStack() as ctx:
         lists = ctx.enter_context(tc.tile_pool(name="lists", bufs=1))
         keep = ctx.enter_context(tc.tile_pool(name="keep", bufs=1))
+        placed = ctx.enter_context(tc.tile_pool(name="placed", bufs=1))
         work = ctx.enter_context(tc.tile_pool(name="work", bufs=2))
         psum = ctx.enter_context(tc.psum_pool(name="psum", bufs=8))
 
@@ -73,13 +77,10 @@ def tile_picked_tricdflowbmaxbmed_none_p_kernel(
         l_n7 = load_list(n7, "l_n7")
         l_n6 = load_list(n6, "l_n6")
 
-        def pick_scales(lst, name, tag=None):
-            dst = keep.tile([P, S], U8, name=name, tag=tag or name, align_bytes=64)
+        def pick_scales(dst, lst):
             nc.vector.tensor_copy(dst[:], table_scales[:].indirect(lst[:]))
-            return dst
 
-        def pick_dealt_scales(lst, name, tag=None):
-            picked = pick_scales(lst, name + "_picked", tag)
+        def deal_scales(picked, name):
             dst = keep.tile([P, S], U8, name=name, align_bytes=64)
             nc.vector.tensor_copy(
                 dst[:].bitcast(I32).rearrange("p (t a) -> p t a", t=TILES),
@@ -87,21 +88,23 @@ def tile_picked_tricdflowbmaxbmed_none_p_kernel(
             )
             return dst
 
-        def pick_dealt_words(lst, name, tag):
-            dst = keep.tile([P, S], U32, name=name, tag=tag, align_bytes=64)
+        def pick_dealt_words(dst, lst):
             nc.vector.tensor_copy(
                 dst[:].rearrange("p (t a v) -> p a t v", t=TILES, v=4), table_words[:].indirect(lst[:])
             )
-            return dst
 
-        token_scales = pick_scales(l_offs, "token_scales")
-        a_scales = pick_dealt_scales(l_ca, "a_scales")
+        token_scales = keep.tile([P, S], U8, name="token_scales", align_bytes=64)
+        a_picked = keep.tile([P, S], U8, name="a_picked", align_bytes=64)
+        b_picked = keep.tile([P, S], U8, name="b_picked", align_bytes=64)
+        pick_scales(token_scales, l_offs)
+        pick_scales(a_picked, l_ca)
+        pick_scales(b_picked, l_cb)
+        a_scales = deal_scales(a_picked, "a_scales")
+        b_scales = deal_scales(b_picked, "b_scales")
 
-        b_scales = pick_dealt_scales(l_cb, "b_scales")
-
-        w_codes = keep.tile([P, H], U32, name="w_codes", align_bytes=64)
-        w_scales = keep.tile([P, H], U8, name="w_scales", align_bytes=64)
-        token_words = keep.tile([P, S], U32, name="token_words", align_bytes=64)
+        w_codes = [keep.tile([P, HALF], U32, name=f"w_codes{g}", align_bytes=64) for g in range(2)]
+        w_scales = [keep.tile([P, HALF], U8, name=f"w_scales{g}", align_bytes=64) for g in range(2)]
+        token_words = [keep.tile([P, HALF], U32, name=f"token_words{g}", align_bytes=64) for g in range(2)]
 
         def quantize_weights(pair):
             w_bf = keep.tile([P, 2, P, PACK], BF16, name="w_bf", tag=f"w_pair{pair}", align_bytes=64)
@@ -110,21 +113,25 @@ def tile_picked_tricdflowbmaxbmed_none_p_kernel(
                 w_raw[:].rearrange("p j (m t) -> p m j t", t=TILES)[:, :, :, 2 * pair : 2 * pair + 2],
             )
             nc.vector.quantize_mx(
-                out=w_codes[:, cols(pair)].bitcast(FP8X4),
-                scales=w_scales[:, cols(pair)],
+                out=w_codes[pair][:].bitcast(FP8X4),
+                scales=w_scales[pair][:],
                 in_=w_bf[:].rearrange("p t m j -> p (t m j)"),
             )
 
         quantize_weights(0)
         for h in range(2):
-            nc.vector.tensor_copy(token_words[:, cols(h)], table_words[:].indirect(half_of(l_offs, h)))
+            nc.vector.tensor_copy(token_words[h][:], table_words[:].indirect(half_of(l_offs, h)))
         quantize_weights(1)
 
-        def product(width, lhs_words, lhs_scales, t, rhs_words, rhs_scales):
-            acc = psum.tile([P, width], F32, name="acc")
-            rows = slice(t * P, (t + 1) * P)
+        def bank(width, linked=False):
+            if linked:
+                return psum.tile([P, width], F32, name="linked", bufs=1)
+            return psum.tile([P, width], F32, name="acc", bufs=7)
+
+        def product(acc, lhs_words, lhs_scales, block, rhs_words, rhs_scales):
+            rows = slice(block * P, (block + 1) * P)
             nc.tensor.matmul_mx(
-                out=acc[:],
+                out=acc,
                 lhsT=lhs_words[:, rows].bitcast(FP8X4),
                 lhsT_scale=lhs_scales[:, rows],
                 rhs=rhs_words.bitcast(FP8X4),
@@ -132,57 +139,87 @@ def tile_picked_tricdflowbmaxbmed_none_p_kernel(
                 start=True,
                 stop=True,
             )
-            return acc
 
-        a_words = pick_dealt_words(l_ca, "a_words", "w_pair0")
-        b_words = pick_dealt_words(l_cb, "b_words", "w_pair1")
+        def project(t, halves):
+            acc = bank(HALF * len(halves))
+            for i, g in enumerate(halves):
+                product(
+                    acc[:, cols(i)], w_codes[t // 2], w_scales[t // 2], t % 2, token_words[g][:], token_scales[:, cols(g)]
+                )
+            nc.scalar.activation(
+                y[t][:, halves[0] * HALF : (halves[-1] + 1) * HALF], acc[:], COPY, scale=gain[:, t : t + 1]
+            )
+
+        a_words = keep.tile([P, S], U32, name="a_words", tag="w_pair0", align_bytes=64)
+        pick_dealt_words(a_words, l_ca)
+        b_words = keep.tile([P, S], U32, name="b_words", tag="w_pair1", align_bytes=64)
+        pick_dealt_words(b_words, l_cb)
 
         y = [keep.tile([P, S], F32, name=f"y{t}") for t in range(TILES)]
-        a = [keep.tile([P, S], F32, name=f"a{t}") for t in range(TILES)]
-        b = [keep.tile([P, S], F32, name=f"b{t}") for t in range(TILES)]
-        q = {}
+        a = [keep.tile([P, 2 * S], F32, name=f"a{t}") for t in range(TILES)]
+        b = [keep.tile([P, 2 * S], F32, name=f"b{t}") for t in range(TILES)]
+        q = [keep.tile([P, 2 * S], F32, name=f"q{t}") for t in range(TILES)]
         z_codes = keep.tile([P, S], U32, name="z_codes", align_bytes=64)
         z_scales = keep.tile([P, S], U8, name="z_scales", align_bytes=64)
 
+        y_bf = keep.tile([P, TILES, S], BF16, name="y_bf")
+
+        def fetch(dst, window, offsets, on_vector):
+            if on_vector:
+                nc.vector.tensor_copy(dst, window[:].indirect(offsets))
+            else:
+                nc.scalar.activation(dst, window[:].indirect(offsets), COPY)
+
         def median_half(h):
-            low = work.tile([P, TILES, HALF], F32, name="low")
-            mid = work.tile([P, TILES, HALF], F32, name="mid")
+            low = work.tile([P, TILES, HALF], BF16, name="low")
+            mid = work.tile([P, TILES, HALF], BF16, name="mid")
+            pa = work.tile([P, TILES, HALF], BF16, name="pa")
+            pb = work.tile([P, TILES, HALF], BF16, name="pb")
+            high = work.tile([P, TILES, HALF], BF16, name="high")
             for t in range(TILES):
                 if h == 0 and t == 0:
-                    for g in range(2):
-                        acc = product(HALF, w_codes, w_scales, t, token_words[:, cols(g)], token_scales[:, cols(g)])
-                        nc.scalar.activation(y[t][:, cols(g)], acc[:], COPY, scale=gain[:, t : t + 1])
+                    project(t, [0])
+                    project(t, [1])
                 elif h == 0:
-                    acc = product(S, w_codes, w_scales, t, token_words[:], token_scales[:])
-                    nc.scalar.activation(y[t][:], acc[:], COPY, scale=gain[:, t : t + 1])
-                pa = work.tile([P, HALF], F32, name="pa", bufs=4)
-                pb = work.tile([P, HALF], F32, name="pb", bufs=4)
-                high = work.tile([P, HALF], F32, name="high")
-                nc.scalar.activation(pa[:], y[t][:].indirect(half_of(l_n1, h)), COPY)
-                if (t, h) in VECTOR_PB:
-                    nc.vector.tensor_copy(pb[:], y[t][:].indirect(half_of(l_n2, h)))
-                else:
-                    nc.scalar.activation(pb[:], y[t][:].indirect(half_of(l_n2, h)), COPY)
-                nc.vector.tensor_tensor(high[:], y[t][:, cols(h)], pa[:], ALU.max)
-                nc.vector.tensor_tensor(low[:, t, :], y[t][:, cols(h)], pa[:], ALU.min)
-                nc.vector.tensor_tensor(mid[:, t, :], high[:], pb[:], ALU.min)
-            z = keep.tile([P, HALF * PACK], BF16, name="z", tag=f"z{h}", align_bytes=64)
-            nc.vector.tensor_tensor(
-                z[:].rearrange("p (c i t) -> p c t i", i=2, t=PACK),
-                low[:].rearrange("p t (c i) -> p c t i", i=2),
-                mid[:].rearrange("p t (c i) -> p c t i", i=2),
-                ALU.max,
-            )
-            nc.vector.quantize_mx(out=z_codes[:, cols(h)].bitcast(FP8X4), scales=z_scales[:, cols(h)], in_=z[:])
+                    project(t, [0, 1])
+                if h == 0:
+                    nc.vector.tensor_copy(y_bf[:, t, :], y[t][:])
+                fetch(pa[:, t, :], y[t], half_of(l_n1, h), False)
+                fetch(pb[:, t, :], y[t], half_of(l_n2, h), (t, h) in VECTOR_PB)
+                if t % GROUP == GROUP - 1:
+                    ts = slice(t + 1 - GROUP, t + 1)
+                    nc.vector.tensor_tensor(high[:, ts, :], y_bf[:, ts, cols(h)], pa[:, ts, :], ALU.max)
+                    nc.vector.tensor_tensor(low[:, ts, :], y_bf[:, ts, cols(h)], pa[:, ts, :], ALU.min)
+                    nc.vector.tensor_tensor(mid[:, ts, :], high[:, ts, :], pb[:, ts, :], ALU.min)
+            z = placed.tile([P, HALF * PACK], BF16, name=f"z{h}", align_bytes=64, offset=4096 * h)
+            width = HALF // Z_PIECES
+            for i in range(Z_PIECES):
+                nc.vector.tensor_tensor(
+                    z[:, i * width * PACK : (i + 1) * width * PACK].rearrange("p (c i t) -> p c t i", i=4, t=PACK),
+                    low[:, :, i * width : (i + 1) * width].rearrange("p t (c i) -> p c t i", i=4),
+                    mid[:, :, i * width : (i + 1) * width].rearrange("p t (c i) -> p c t i", i=4),
+                    ALU.max,
+                )
+            for i in range(Z_PIECES):
+                piece = slice(h * HALF + i * width, h * HALF + (i + 1) * width)
+                nc.vector.quantize_mx(
+                    out=z_codes[:, piece].bitcast(FP8X4),
+                    scales=z_scales[:, piece],
+                    in_=z[:, i * width * PACK : (i + 1) * width * PACK],
+                )
 
-        def score(dst, words, scales, t, h):
-            acc = product(HALF, words, scales, t, z_codes[:, cols(h)], z_scales[:, cols(h)])
+        def score(dst, words, scales, t, h, linked=False):
+            acc = bank(HALF, linked)
+            product(acc[:], words, scales, t, z_codes[:, cols(h)], z_scales[:, cols(h)])
             nc.scalar.activation(dst[t][:, cols(h)], acc[:], COPY, scale=SCORE_SCALE)
 
         median_half(0)
         median_half(1)
-        q_scales = pick_dealt_scales(l_cd, "q_scales", "z1")
-        q_words = pick_dealt_words(l_cd, "q_words", "z1")
+        q_picked = placed.tile([P, S], U8, name="q_picked", align_bytes=64, offset=4096 + 1024)
+        q_words = placed.tile([P, S], U32, name="q_words", align_bytes=64, offset=4096 + 1536)
+        pick_scales(q_picked, l_cd)
+        pick_dealt_words(q_words, l_cd)
+        q_scales = deal_scales(q_picked, "q_scales")
         for t in range(TILES):
             score(a, a_words, a_scales, t, 0)
             score(b, b_words, b_scales, t, 0)
@@ -191,51 +228,75 @@ def tile_picked_tricdflowbmaxbmed_none_p_kernel(
         m1 = {}
         upper = [keep.tile([P, S], F32, name=f"upper{t}") for t in range(TILES)]
 
+        def fetch_row(dst, window, lst, vector_halves):
+            if len(vector_halves) == 1:
+                for h in range(2):
+                    fetch(dst[:, cols(h)], window, half_of(lst, h), h in vector_halves)
+            else:
+                fetch(dst[:], window, lst[:], len(vector_halves) == 2)
+
+        whole = [slice(0, S)]
+        halves = [cols(0), cols(1)]
+
         def flows(t):
-            score(a, a_words, a_scales, t, 1)
-            score(b, b_words, b_scales, t, 1)
+            last = t == TILES - 1
             a3 = work.tile([P, S], F32, name="a3")
             a4 = work.tile([P, S], F32, name="a4", bufs=1)
             d3 = work.tile([P, S], F32, name="d3")
             d4 = work.tile([P, S], F32, name="d4")
             e3 = work.tile([P, S], F32, name="e3")
-            e4 = work.tile([P, S], F32, name="e4")
-            q7 = work.tile([P, S], F32, name="q7")
+            e4 = work.tile([P, S], F32, name="e4", bufs=1)
+            b5 = work.tile([P, S], F32, name="b5")
+            fetch_row(a4, a[t], l_n4, [])
             for h in range(2):
-                nc.scalar.activation(a4[:, cols(h)], a[t][:].indirect(half_of(l_n4, h)), COPY)
-            for h in range(2):
-                fetch(a3, a[t], l_n3, h, (t, h) in VECTOR_A3)
+                if (t, h) in SCALAR_B5:
+                    fetch(b5[:, cols(h)], b[t], half_of(l_n5, h), False)
+            fetch_row(a3, a[t], l_n3, [h for h in range(2) if (t, h) in VECTOR_A3])
+            acc = bank(S, True)
+            product(acc[:], q_words, q_scales, t, z_codes[:], z_scales[:])
+            nc.scalar.activation(q[t][:, :S], acc[:], COPY, scale=SCORE_SCALE)
             if t > 0:
                 fetch_m6(t - 1)
-            q[t] = keep.tile([P, S], F32, name=f"q{t}", tag=f"chain{t}")
-            for h in range(2):
-                score(q, q_words, q_scales, t, h)
-            for h in range(2):
-                nc.scalar.activation(q7[:, cols(h)], q[t][:].indirect(half_of(l_n7, h)), COPY)
-            nc.vector.tensor_tensor(d4[:], a4[:], a[t][:], ALU.subtract)
-            for h in range(2):
-                nc.vector.tensor_tensor(e4[:, cols(h)], b[t][:].indirect(half_of(l_n5, h)), d4[:, cols(h)], ALU.mult)
-            nc.vector.tensor_tensor(d3[:], a3[:], a[t][:], ALU.subtract)
-            if t > 0:
-                finish(t - 1, [slice(0, S)])
-            nc.vector.tensor_tensor(e3[:], d3[:], b[t][:], ALU.mult)
-            m1[t] = keep.tile([P, S], F32, name=f"m1_{t}", tag=f"chain{t + 1}")
-            nc.vector.scalar_tensor_tensor(m1[t][:], e4[:], 0.5, e3[:], ALU.mult, ALU.add)
-            nc.vector.tensor_tensor(upper[t][:], m1[t][:], q7[:], ALU.max)
-
-        def fetch(dst, window, lst, h, on_vector):
-            if on_vector:
-                nc.vector.tensor_copy(dst[:, cols(h)], window[:].indirect(half_of(lst, h)))
+            if not last:
+                score(a, a_words, a_scales, t + 1, 1, True)
+                score(b, b_words, b_scales, t + 1, 1)
+            q7 = keep.tile([P, S], F32, name="q7", tag=f"chain{t}")
+            fetch_row(q7, q[t], l_n7, [])
+            nc.vector.tensor_tensor(d4[:], a4[:], a[t][:, :S], ALU.subtract)
+            if (t, 0) in SCALAR_B5 or (t, 1) in SCALAR_B5:
+                for h in range(2):
+                    if (t, h) in SCALAR_B5:
+                        nc.vector.tensor_tensor(e4[:, cols(h)], b5[:, cols(h)], d4[:, cols(h)], ALU.mult)
+                    else:
+                        nc.vector.tensor_tensor(
+                            e4[:, cols(h)], b[t][:].indirect(half_of(l_n5, h)), d4[:, cols(h)], ALU.mult
+                        )
             else:
-                nc.scalar.activation(dst[:, cols(h)], window[:].indirect(half_of(lst, h)), COPY)
+                nc.vector.tensor_tensor(e4[:], b[t][:].indirect(l_n5[:]), d4[:], ALU.mult)
+            pieces = halves if last else whole
+            for piece in pieces:
+                nc.vector.tensor_tensor(d3[:, piece], a3[:, piece], a[t][:, piece], ALU.subtract)
+            if t > 0 and not last:
+                finish(t - 1, whole, "lower")
+            for piece in pieces:
+                nc.vector.tensor_tensor(e3[:, piece], d3[:, piece], b[t][:, piece], ALU.mult)
+            m1[t] = keep.tile([P, 2 * S], F32, name=f"m1_{t}", tag=f"chain{t + 1}")
+            for piece in pieces:
+                nc.vector.scalar_tensor_tensor(m1[t][:, piece], e4[:, piece], 0.5, e3[:, piece], ALU.mult, ALU.add)
+            if last:
+                finish(t - 1, whole, "e4")
+            nc.vector.tensor_tensor(upper[t][:], m1[t][:, :S], q7[:], ALU.max)
 
         def fetch_m6(t):
             m6[t] = work.tile([P, S], F32, name="m6")
-            for h in range(2):
-                fetch(m6[t], m1[t], l_n6, h, (t, h) in VECTOR_M6)
+            if t == TILES - 1:
+                for h in range(2):
+                    fetch(m6[t][:, cols(h)], m1[t], half_of(l_n6, h), (t, h) in VECTOR_M6)
+            else:
+                fetch_row(m6[t], m1[t], l_n6, [h for h in range(2) if (t, h) in VECTOR_M6])
 
-        def finish(t, pieces):
-            lower = work.tile([P, S], F32, name="lower")
+        def finish(t, pieces, tag):
+            lower = work.tile([P, S], F32, name="lower", tag=tag, bufs=1)
             res = work.tile([P, S], F32, name="res")
             for piece in pieces:
                 nc.vector.tensor_tensor(lower[:, piece], m6[t][:, piece], q[t][:, piece], ALU.min)
@@ -244,7 +305,9 @@ def tile_picked_tricdflowbmaxbmed_none_p_kernel(
                 nc.sync.dma_start(out_rows[t][:, :, piece], res[:, piece])
 
         m6 = {}
+        score(a, a_words, a_scales, 0, 1, True)
+        score(b, b_words, b_scales, 0, 1)
         for t in range(TILES):
             flows(t)
         fetch_m6(TILES - 1)
-        finish(TILES - 1, [cols(0), cols(1)])
+        finish(TILES - 1, halves, "lower")

@@ -24,8 +24,15 @@ GROUP = 2
 Z_PIECES = 2
 VECTOR_PB = [(0, 0), (1, 0), (2, 0), (3, 0)]
 VECTOR_A3 = []
-VECTOR_M6 = [(0, 0)]
-SCALAR_B5 = [(3, 1)]
+VECTOR_M6 = []
+SCALAR_B5 = []
+POOL_RES = []
+SHARE_A3 = [256, 256, 256, 0]
+SHARE_B5 = [512, 512, 512, 512]
+POOL_E4 = [0, 1, 2, 3]
+A4_BUFS = 1
+POOL_M1 = [0, 1, 2]
+KEPT = 2
 
 
 def tile_picked_tricdflowbmaxbmed_none_p_kernel(
@@ -37,7 +44,7 @@ def tile_picked_tricdflowbmaxbmed_none_p_kernel(
         keep = ctx.enter_context(tc.tile_pool(name="keep", bufs=1))
         placed = ctx.enter_context(tc.tile_pool(name="placed", bufs=1))
         work = ctx.enter_context(tc.tile_pool(name="work", bufs=2))
-        psum = ctx.enter_context(tc.psum_pool(name="psum", bufs=8))
+        psum = ctx.enter_context(tc.psum_pool(name="psum", bufs=2))
 
         def load_list(src, name):
             dst = lists.tile([P, S // 16], U16, name=name)
@@ -104,10 +111,9 @@ def tile_picked_tricdflowbmaxbmed_none_p_kernel(
 
         w_codes = [keep.tile([P, HALF], U32, name=f"w_codes{g}", align_bytes=64) for g in range(2)]
         w_scales = [keep.tile([P, HALF], U8, name=f"w_scales{g}", align_bytes=64) for g in range(2)]
-        token_words = [keep.tile([P, HALF], U32, name=f"token_words{g}", align_bytes=64) for g in range(2)]
 
         def quantize_weights(pair):
-            w_bf = keep.tile([P, 2, P, PACK], BF16, name="w_bf", tag=f"w_pair{pair}", align_bytes=64)
+            w_bf = placed.tile([P, 2, P, PACK], BF16, name=f"w_bf{pair}", align_bytes=64, offset=4096 * pair)
             nc.scalar.copy(
                 w_bf[:].rearrange("p t m j -> p m j t"),
                 w_raw[:].rearrange("p j (m t) -> p m j t", t=TILES)[:, :, :, 2 * pair : 2 * pair + 2],
@@ -119,14 +125,15 @@ def tile_picked_tricdflowbmaxbmed_none_p_kernel(
             )
 
         quantize_weights(0)
+        token_words = [
+            placed.tile([P, HALF], U32, name=f"token_words{g}", align_bytes=64, offset=1024 * g) for g in range(2)
+        ]
         for h in range(2):
             nc.vector.tensor_copy(token_words[h][:], table_words[:].indirect(half_of(l_offs, h)))
         quantize_weights(1)
 
-        def bank(width, linked=False):
-            if linked:
-                return psum.tile([P, width], F32, name="linked", bufs=1)
-            return psum.tile([P, width], F32, name="acc", bufs=7)
+        def bank(width, ring):
+            return psum.tile([P, width], F32, name=ring)
 
         def product(acc, lhs_words, lhs_scales, block, rhs_words, rhs_scales):
             rows = slice(block * P, (block + 1) * P)
@@ -141,7 +148,7 @@ def tile_picked_tricdflowbmaxbmed_none_p_kernel(
             )
 
         def project(t, halves):
-            acc = bank(HALF * len(halves))
+            acc = bank(HALF * len(halves), ("early", "q", "q", "a")[t])
             for i, g in enumerate(halves):
                 product(
                     acc[:, cols(i)], w_codes[t // 2], w_scales[t // 2], t % 2, token_words[g][:], token_scales[:, cols(g)]
@@ -150,9 +157,9 @@ def tile_picked_tricdflowbmaxbmed_none_p_kernel(
                 y[t][:, halves[0] * HALF : (halves[-1] + 1) * HALF], acc[:], COPY, scale=gain[:, t : t + 1]
             )
 
-        a_words = keep.tile([P, S], U32, name="a_words", tag="w_pair0", align_bytes=64)
+        a_words = placed.tile([P, S], U32, name="a_words", align_bytes=64, offset=3072)
         pick_dealt_words(a_words, l_ca)
-        b_words = keep.tile([P, S], U32, name="b_words", tag="w_pair1", align_bytes=64)
+        b_words = placed.tile([P, S], U32, name="b_words", align_bytes=64, offset=5120)
         pick_dealt_words(b_words, l_cb)
 
         y = [keep.tile([P, S], F32, name=f"y{t}") for t in range(TILES)]
@@ -191,7 +198,7 @@ def tile_picked_tricdflowbmaxbmed_none_p_kernel(
                     nc.vector.tensor_tensor(high[:, ts, :], y_bf[:, ts, cols(h)], pa[:, ts, :], ALU.max)
                     nc.vector.tensor_tensor(low[:, ts, :], y_bf[:, ts, cols(h)], pa[:, ts, :], ALU.min)
                     nc.vector.tensor_tensor(mid[:, ts, :], high[:, ts, :], pb[:, ts, :], ALU.min)
-            z = placed.tile([P, HALF * PACK], BF16, name=f"z{h}", align_bytes=64, offset=4096 * h)
+            z = placed.tile([P, HALF * PACK], BF16, name=f"z{h}", align_bytes=64, offset=8192 + 4096 * h)
             width = HALF // Z_PIECES
             for i in range(Z_PIECES):
                 nc.vector.tensor_tensor(
@@ -208,25 +215,36 @@ def tile_picked_tricdflowbmaxbmed_none_p_kernel(
                     in_=z[:, i * width * PACK : (i + 1) * width * PACK],
                 )
 
-        def score(dst, words, scales, t, h, linked=False):
-            acc = bank(HALF, linked)
-            product(acc[:], words, scales, t, z_codes[:, cols(h)], z_scales[:, cols(h)])
-            nc.scalar.activation(dst[t][:, cols(h)], acc[:], COPY, scale=SCORE_SCALE)
+        banks = {}
+
+        def score(name, dst, words, scales, t, halves, evacuate):
+            if (name, t) not in banks:
+                banks[name, t] = bank(S, "early" if t >= KEPT and halves == [0] else name)
+            acc = banks[name, t]
+            span = slice(halves[0] * HALF, (halves[-1] + 1) * HALF)
+            product(acc[:, span], words, scales, t, z_codes[:, span], z_scales[:, span])
+            nc.scalar.activation(dst[t][:, evacuate], acc[:, evacuate], COPY, scale=SCORE_SCALE)
 
         median_half(0)
         median_half(1)
-        q_picked = placed.tile([P, S], U8, name="q_picked", align_bytes=64, offset=4096 + 1024)
-        q_words = placed.tile([P, S], U32, name="q_words", align_bytes=64, offset=4096 + 1536)
+        q_picked = placed.tile([P, S], U8, name="q_picked", align_bytes=64, offset=12288 + 1024)
+        q_words = placed.tile([P, S], U32, name="q_words", align_bytes=64, offset=12288 + 1536)
         pick_scales(q_picked, l_cd)
         pick_dealt_words(q_words, l_cd)
         q_scales = deal_scales(q_picked, "q_scales")
         for t in range(TILES):
-            score(a, a_words, a_scales, t, 0)
-            score(b, b_words, b_scales, t, 0)
+            score("a", a, a_words, a_scales, t, [0], cols(0))
+            score("b", b, b_words, b_scales, t, [0], cols(0))
+            if t >= KEPT:
+                banks.pop(("a", t))
+                banks.pop(("b", t))
 
         out_rows = out.rearrange("(a t v) c -> t a v c", t=TILES, v=4)
         m1 = {}
+        m6 = {}
         upper = [keep.tile([P, S], F32, name=f"upper{t}") for t in range(TILES)]
+        whole = [slice(0, S)]
+        halves = [cols(0), cols(1)]
 
         def fetch_row(dst, window, lst, vector_halves):
             if len(vector_halves) == 1:
@@ -235,79 +253,82 @@ def tile_picked_tricdflowbmaxbmed_none_p_kernel(
             else:
                 fetch(dst[:], window, lst[:], len(vector_halves) == 2)
 
-        whole = [slice(0, S)]
-        halves = [cols(0), cols(1)]
+        def second_scores(t):
+            score("a", a, a_words, a_scales, t, [1] if t < KEPT else [0, 1], cols(1))
+            score("b", b, b_words, b_scales, t, [1] if t < KEPT else [0, 1], cols(1))
 
-        def flows(t):
-            last = t == TILES - 1
+        q7 = {}
+        last = TILES - 1
+
+        def fetch_shared(dst, window, lst, share, scale=1.0):
+            split = S - share
+            if split > 0:
+                nc.scalar.activation(dst[:, :split], window[:].indirect(lst[:, : split // 16]), COPY, scale=scale)
+            if split < S:
+                fetch(dst[:, split:], window, lst[:, split // 16 :], True)
+
+        def flow(t):
             a3 = work.tile([P, S], F32, name="a3")
-            a4 = work.tile([P, S], F32, name="a4", bufs=1)
+            a4 = work.tile([P, S], F32, name="a4")
+            b5 = work.tile([P, S], F32, name="b5")
             d3 = work.tile([P, S], F32, name="d3")
             d4 = work.tile([P, S], F32, name="d4")
             e3 = work.tile([P, S], F32, name="e3")
-            e4 = work.tile([P, S], F32, name="e4", bufs=1)
-            b5 = work.tile([P, S], F32, name="b5")
-            fetch_row(a4, a[t], l_n4, [])
-            for h in range(2):
-                if (t, h) in SCALAR_B5:
-                    fetch(b5[:, cols(h)], b[t], half_of(l_n5, h), False)
-            fetch_row(a3, a[t], l_n3, [h for h in range(2) if (t, h) in VECTOR_A3])
-            acc = bank(S, True)
-            product(acc[:], q_words, q_scales, t, z_codes[:], z_scales[:])
-            nc.scalar.activation(q[t][:, :S], acc[:], COPY, scale=SCORE_SCALE)
-            if t > 0:
-                fetch_m6(t - 1)
-            if not last:
-                score(a, a_words, a_scales, t + 1, 1, True)
-                score(b, b_words, b_scales, t + 1, 1)
-            q7 = keep.tile([P, S], F32, name="q7", tag=f"chain{t}")
-            fetch_row(q7, q[t], l_n7, [])
-            nc.vector.tensor_tensor(d4[:], a4[:], a[t][:, :S], ALU.subtract)
-            if (t, 0) in SCALAR_B5 or (t, 1) in SCALAR_B5:
-                for h in range(2):
-                    if (t, h) in SCALAR_B5:
-                        nc.vector.tensor_tensor(e4[:, cols(h)], b5[:, cols(h)], d4[:, cols(h)], ALU.mult)
-                    else:
-                        nc.vector.tensor_tensor(
-                            e4[:, cols(h)], b[t][:].indirect(half_of(l_n5, h)), d4[:, cols(h)], ALU.mult
-                        )
-            else:
-                nc.vector.tensor_tensor(e4[:], b[t][:].indirect(l_n5[:]), d4[:], ALU.mult)
-            pieces = halves if last else whole
+            e4 = work.tile([P, S], F32, name="e4")
+            m1[t] = keep.tile([P, 2 * S], F32, name=f"m1_{t}")
+            fetch_shared(a4, a[t], l_n4, 0, 0.5)
+            fetch_shared(a3, a[t], l_n3, SHARE_A3[t])
+            fetch_shared(b5, b[t], l_n5, SHARE_B5[t])
+            nc.vector.scalar_tensor_tensor(d4[:], banks["a", t][:], -0.5 * SCORE_SCALE, a4[:], ALU.mult, ALU.add)
+            (nc.gpsimd if t in POOL_E4 else nc.vector).tensor_tensor(e4[:], b5[:], d4[:], ALU.mult)
+            pieces = halves if t == last else whole
             for piece in pieces:
-                nc.vector.tensor_tensor(d3[:, piece], a3[:, piece], a[t][:, piece], ALU.subtract)
-            if t > 0 and not last:
-                finish(t - 1, whole, "lower")
+                nc.vector.scalar_tensor_tensor(
+                    d3[:, piece], banks["a", t][:, piece], -SCORE_SCALE, a3[:, piece], ALU.mult, ALU.add
+                )
             for piece in pieces:
-                nc.vector.tensor_tensor(e3[:, piece], d3[:, piece], b[t][:, piece], ALU.mult)
-            m1[t] = keep.tile([P, 2 * S], F32, name=f"m1_{t}", tag=f"chain{t + 1}")
+                nc.vector.scalar_tensor_tensor(
+                    e3[:, piece], banks["b", t][:, piece], SCORE_SCALE, d3[:, piece], ALU.mult, ALU.mult
+                )
             for piece in pieces:
-                nc.vector.scalar_tensor_tensor(m1[t][:, piece], e4[:, piece], 0.5, e3[:, piece], ALU.mult, ALU.add)
-            if last:
-                finish(t - 1, whole, "e4")
-            nc.vector.tensor_tensor(upper[t][:], m1[t][:, :S], q7[:], ALU.max)
+                engine = nc.gpsimd if t in POOL_M1 else nc.vector
+                engine.tensor_tensor(m1[t][:, piece], e4[:, piece], e3[:, piece], ALU.add)
+
+        def fetch_q7(t):
+            score("q", q, q_words, q_scales, t, [0, 1], slice(0, S))
+            q7[t] = work.tile([P, S], F32, name="q7")
+            fetch(q7[t][:], q[t], l_n7[:], False)
 
         def fetch_m6(t):
             m6[t] = work.tile([P, S], F32, name="m6")
-            if t == TILES - 1:
+            if t == last:
                 for h in range(2):
-                    fetch(m6[t][:, cols(h)], m1[t], half_of(l_n6, h), (t, h) in VECTOR_M6)
+                    fetch(m6[t][:, cols(h)], m1[t], half_of(l_n6, h), False)
             else:
-                fetch_row(m6[t], m1[t], l_n6, [h for h in range(2) if (t, h) in VECTOR_M6])
+                fetch(m6[t][:], m1[t], l_n6[:], False)
 
-        def finish(t, pieces, tag):
-            lower = work.tile([P, S], F32, name="lower", tag=tag, bufs=1)
+        def finish(t, pieces, engine):
+            lower = work.tile([P, S], F32, name="lower")
             res = work.tile([P, S], F32, name="res")
+            nc.vector.tensor_tensor(upper[t][:], m1[t][:, :S], q7[t][:], ALU.max)
             for piece in pieces:
-                nc.vector.tensor_tensor(lower[:, piece], m6[t][:, piece], q[t][:, piece], ALU.min)
+                nc.vector.scalar_tensor_tensor(
+                    lower[:, piece], banks["q", t][:, piece], SCORE_SCALE, m6[t][:, piece], ALU.mult, ALU.min
+                )
             for piece in pieces:
-                nc.vector.tensor_tensor(res[:, piece], upper[t][:, piece], lower[:, piece], ALU.subtract)
+                engine.tensor_tensor(res[:, piece], upper[t][:, piece], lower[:, piece], ALU.subtract)
                 nc.sync.dma_start(out_rows[t][:, :, piece], res[:, piece])
 
-        m6 = {}
-        score(a, a_words, a_scales, 0, 1, True)
-        score(b, b_words, b_scales, 0, 1)
+        second_scores(0)
+        second_scores(1)
         for t in range(TILES):
-            flows(t)
-        fetch_m6(TILES - 1)
-        finish(TILES - 1, halves, "lower")
+            flow(t)
+            if t > 0:
+                fetch_m6(t - 1)
+            fetch_q7(t)
+            if t + 2 < TILES:
+                second_scores(t + 2)
+            if t > 0:
+                finish(t - 1, whole, nc.gpsimd if t - 1 in POOL_RES else nc.vector)
+        fetch_m6(last)
+        finish(last, halves, nc.vector)

@@ -2,7 +2,7 @@ from contextlib import ExitStack
 
 import concourse.mybir as mybir
 
-K, T, S, H, C = 512, 2048, 512, 512, 512
+T, S, H = 2048, 512, 512
 FLOPS = 4 * 2 * 512 * 512 * 512
 
 F32 = mybir.dt.float32
@@ -18,21 +18,21 @@ COPY = mybir.ActivationFunctionType.Copy
 P = 128
 PACK = 4
 TILES = 4
+LAST = TILES - 1
 HALF = S // 2
+QUARTER = S // 4
+STRIPE = 16
+RUN = 4
 SCORE_SCALE = 0.0625
-GROUP = 2
-Z_PIECES = 2
-VECTOR_PB = [(0, 0), (1, 0), (2, 0), (3, 0)]
-VECTOR_A3 = []
-VECTOR_M6 = []
-SCALAR_B5 = []
-POOL_RES = []
-SHARE_A3 = [256, 256, 256, 0]
-SHARE_B5 = [512, 512, 512, 512]
-POOL_E4 = [0, 1, 2, 3]
-A4_BUFS = 1
-POOL_M1 = [0, 1, 2]
-KEPT = 2
+SHARED = 2
+
+AT_W_BF = (2048, 6144)
+AT_A_WORDS = 512
+AT_TOKEN_WORDS = (2560, 3584)
+AT_B_WORDS = 5120
+AT_Z = (8192, 12288)
+AT_Q_PICKED = 12288
+AT_Q_WORDS = 13312
 
 
 def tile_picked_tricdflowbmaxbmed_none_p_kernel(
@@ -44,18 +44,21 @@ def tile_picked_tricdflowbmaxbmed_none_p_kernel(
         keep = ctx.enter_context(tc.tile_pool(name="keep", bufs=1))
         placed = ctx.enter_context(tc.tile_pool(name="placed", bufs=1))
         work = ctx.enter_context(tc.tile_pool(name="work", bufs=2))
-        psum = ctx.enter_context(tc.psum_pool(name="psum", bufs=2))
+        psum = ctx.enter_context(tc.psum_pool(name="psum", bufs=1))
 
         def load_list(src, name):
-            dst = lists.tile([P, S // 16], U16, name=name)
+            dst = lists.tile([P, S // STRIPE], U16, name=name)
             nc.sync.dma_start(dst[:], src)
             return dst
 
         def cols(h):
             return slice(h * HALF, (h + 1) * HALF)
 
-        def half_of(lst, h):
-            return lst[:, h * HALF // 16 : (h + 1) * HALF // 16]
+        def entries(lst, span):
+            return lst[:, span.start // STRIPE : span.stop // STRIPE]
+
+        whole = slice(0, S)
+        halves = [cols(0), cols(1)]
 
         l_offs = load_list(offs, "l_offs")
         l_ca = load_list(ca, "l_ca")
@@ -70,9 +73,7 @@ def tile_picked_tricdflowbmaxbmed_none_p_kernel(
         w_raw = keep.tile([P, PACK, H], F32, name="w_raw")
         nc.sync.dma_start(w_raw[:], w1.rearrange("(p j) c -> p j c", j=PACK))
         table_words = keep.tile([P, T], U32, name="table_words", align_bytes=64)
-        nc.sync.dma_start(
-            table_words[:].bitcast(I32), x_words[0].rearrange("p n r -> p (n r)").bitcast(I32)
-        )
+        nc.sync.dma_start(table_words[:].bitcast(I32), x_words[0].rearrange("p n r -> p (n r)").bitcast(I32))
         gain = keep.tile([P, TILES], F32, name="gain")
         nc.sync.dma_start(gain[:], gs.rearrange("(p t) o -> p (t o)", t=TILES))
         l_n1 = load_list(n1, "l_n1")
@@ -90,14 +91,14 @@ def tile_picked_tricdflowbmaxbmed_none_p_kernel(
         def deal_scales(picked, name):
             dst = keep.tile([P, S], U8, name=name, align_bytes=64)
             nc.vector.tensor_copy(
-                dst[:].bitcast(I32).rearrange("p (t a) -> p t a", t=TILES),
-                picked[:].bitcast(I32).rearrange("p (a t) -> p t a", t=TILES),
+                dst[:].bitcast(I32).rearrange("p (t g) -> p t g", t=TILES),
+                picked[:].bitcast(I32).rearrange("p (g t) -> p t g", t=TILES),
             )
             return dst
 
         def pick_dealt_words(dst, lst):
             nc.vector.tensor_copy(
-                dst[:].rearrange("p (t a v) -> p a t v", t=TILES, v=4), table_words[:].indirect(lst[:])
+                dst[:].rearrange("p (t g v) -> p g t v", t=TILES, v=RUN), table_words[:].indirect(lst[:])
             )
 
         token_scales = keep.tile([P, S], U8, name="token_scales", align_bytes=64)
@@ -109,11 +110,11 @@ def tile_picked_tricdflowbmaxbmed_none_p_kernel(
         a_scales = deal_scales(a_picked, "a_scales")
         b_scales = deal_scales(b_picked, "b_scales")
 
-        w_codes = [keep.tile([P, HALF], U32, name=f"w_codes{g}", align_bytes=64) for g in range(2)]
-        w_scales = [keep.tile([P, HALF], U8, name=f"w_scales{g}", align_bytes=64) for g in range(2)]
+        w_codes = [keep.tile([P, HALF], U32, name=f"w_codes{pair}", align_bytes=64) for pair in range(2)]
+        w_scales = [keep.tile([P, HALF], U8, name=f"w_scales{pair}", align_bytes=64) for pair in range(2)]
 
         def quantize_weights(pair):
-            w_bf = placed.tile([P, 2, P, PACK], BF16, name=f"w_bf{pair}", align_bytes=64, offset=4096 * pair)
+            w_bf = placed.tile([P, 2, P, PACK], BF16, name=f"w_bf{pair}", align_bytes=64, offset=AT_W_BF[pair])
             nc.scalar.copy(
                 w_bf[:].rearrange("p t m j -> p m j t"),
                 w_raw[:].rearrange("p j (m t) -> p m j t", t=TILES)[:, :, :, 2 * pair : 2 * pair + 2],
@@ -126,14 +127,14 @@ def tile_picked_tricdflowbmaxbmed_none_p_kernel(
 
         quantize_weights(0)
         token_words = [
-            placed.tile([P, HALF], U32, name=f"token_words{g}", align_bytes=64, offset=1024 * g) for g in range(2)
+            placed.tile([P, HALF], U32, name=f"token_words{h}", align_bytes=64, offset=AT_TOKEN_WORDS[h])
+            for h in range(2)
         ]
         for h in range(2):
-            nc.vector.tensor_copy(token_words[h][:], table_words[:].indirect(half_of(l_offs, h)))
+            nc.vector.tensor_copy(token_words[h][:], table_words[:].indirect(entries(l_offs, cols(h))))
         quantize_weights(1)
-
-        def bank(width, ring):
-            return psum.tile([P, width], F32, name=ring)
+        a_words = placed.tile([P, S], U32, name="a_words", align_bytes=64, offset=AT_A_WORDS)
+        pick_dealt_words(a_words, l_ca)
 
         def product(acc, lhs_words, lhs_scales, block, rhs_words, rhs_scales):
             rows = slice(block * P, (block + 1) * P)
@@ -147,20 +148,11 @@ def tile_picked_tricdflowbmaxbmed_none_p_kernel(
                 stop=True,
             )
 
-        def project(t, halves):
-            acc = bank(HALF * len(halves), ("early", "q", "q", "a")[t])
-            for i, g in enumerate(halves):
-                product(
-                    acc[:, cols(i)], w_codes[t // 2], w_scales[t // 2], t % 2, token_words[g][:], token_scales[:, cols(g)]
-                )
-            nc.scalar.activation(
-                y[t][:, halves[0] * HALF : (halves[-1] + 1) * HALF], acc[:], COPY, scale=gain[:, t : t + 1]
-            )
+        def fetch_on_scalar(dst, window, lst, span):
+            nc.scalar.activation(dst, window[:].indirect(entries(lst, span)), COPY)
 
-        a_words = placed.tile([P, S], U32, name="a_words", align_bytes=64, offset=3072)
-        pick_dealt_words(a_words, l_ca)
-        b_words = placed.tile([P, S], U32, name="b_words", align_bytes=64, offset=5120)
-        pick_dealt_words(b_words, l_cb)
+        def fetch_on_vector(dst, window, lst, span):
+            nc.vector.tensor_copy(dst, window[:].indirect(entries(lst, span)))
 
         y = [keep.tile([P, S], F32, name=f"y{t}") for t in range(TILES)]
         a = [keep.tile([P, 2 * S], F32, name=f"a{t}") for t in range(TILES)]
@@ -168,167 +160,154 @@ def tile_picked_tricdflowbmaxbmed_none_p_kernel(
         q = [keep.tile([P, 2 * S], F32, name=f"q{t}") for t in range(TILES)]
         z_codes = keep.tile([P, S], U32, name="z_codes", align_bytes=64)
         z_scales = keep.tile([P, S], U8, name="z_scales", align_bytes=64)
-
         y_bf = keep.tile([P, TILES, S], BF16, name="y_bf")
 
-        def fetch(dst, window, offsets, on_vector):
-            if on_vector:
-                nc.vector.tensor_copy(dst, window[:].indirect(offsets))
-            else:
-                nc.scalar.activation(dst, window[:].indirect(offsets), COPY)
+        def project(t, token_halves):
+            acc = psum.tile([P, HALF * len(token_halves)], F32, name="acc", bufs=7)
+            for i, h in enumerate(token_halves):
+                product(
+                    acc[:, cols(i)], w_codes[t // 2], w_scales[t // 2], t % 2, token_words[h][:], token_scales[:, cols(h)]
+                )
+            span = slice(token_halves[0] * HALF, (token_halves[-1] + 1) * HALF)
+            nc.scalar.activation(y[t][:, span], acc[:], COPY, scale=gain[:, t : t + 1])
 
-        def median_half(h):
-            low = work.tile([P, TILES, HALF], BF16, name="low")
-            mid = work.tile([P, TILES, HALF], BF16, name="mid")
-            pa = work.tile([P, TILES, HALF], BF16, name="pa")
-            pb = work.tile([P, TILES, HALF], BF16, name="pb")
-            high = work.tile([P, TILES, HALF], BF16, name="high")
-            for t in range(TILES):
-                if h == 0 and t == 0:
-                    project(t, [0])
-                    project(t, [1])
-                elif h == 0:
-                    project(t, [0, 1])
-                if h == 0:
-                    nc.vector.tensor_copy(y_bf[:, t, :], y[t][:])
-                fetch(pa[:, t, :], y[t], half_of(l_n1, h), False)
-                fetch(pb[:, t, :], y[t], half_of(l_n2, h), (t, h) in VECTOR_PB)
-                if t % GROUP == GROUP - 1:
-                    ts = slice(t + 1 - GROUP, t + 1)
-                    nc.vector.tensor_tensor(high[:, ts, :], y_bf[:, ts, cols(h)], pa[:, ts, :], ALU.max)
-                    nc.vector.tensor_tensor(low[:, ts, :], y_bf[:, ts, cols(h)], pa[:, ts, :], ALU.min)
-                    nc.vector.tensor_tensor(mid[:, ts, :], high[:, ts, :], pb[:, ts, :], ALU.min)
-            z = placed.tile([P, HALF * PACK], BF16, name=f"z{h}", align_bytes=64, offset=8192 + 4096 * h)
-            width = HALF // Z_PIECES
-            for i in range(Z_PIECES):
+        low, mid, pa, pb, high = (
+            [work.tile([P, TILES, HALF], BF16, name=name) for h in range(2)]
+            for name in ("low", "mid", "pa", "pb", "high")
+        )
+        quarters = [slice(i * QUARTER, (i + 1) * QUARTER) for i in range(2)]
+
+        def order_pair(h, pair):
+            ts = slice(2 * pair, 2 * pair + 2)
+            nc.vector.tensor_tensor(high[h][:, ts, :], y_bf[:, ts, cols(h)], pa[h][:, ts, :], ALU.max)
+            nc.vector.tensor_tensor(low[h][:, ts, :], y_bf[:, ts, cols(h)], pa[h][:, ts, :], ALU.min)
+            for piece in quarters if pair == 1 else [slice(0, HALF)]:
+                nc.vector.tensor_tensor(mid[h][:, ts, piece], high[h][:, ts, piece], pb[h][:, ts, piece], ALU.min)
+
+        def quantize_z(h):
+            z = placed.tile([P, 2, QUARTER * PACK], BF16, name=f"z{h}", align_bytes=64, offset=AT_Z[h])
+            for i, piece in enumerate(quarters):
                 nc.vector.tensor_tensor(
-                    z[:, i * width * PACK : (i + 1) * width * PACK].rearrange("p (c i t) -> p c t i", i=4, t=PACK),
-                    low[:, :, i * width : (i + 1) * width].rearrange("p t (c i) -> p c t i", i=4),
-                    mid[:, :, i * width : (i + 1) * width].rearrange("p t (c i) -> p c t i", i=4),
+                    z[:, i, :].rearrange("p (c n t) -> p c t n", n=4, t=PACK),
+                    low[h][:, :, piece].rearrange("p t (c n) -> p c t n", n=4),
+                    mid[h][:, :, piece].rearrange("p t (c n) -> p c t n", n=4),
                     ALU.max,
                 )
-            for i in range(Z_PIECES):
-                piece = slice(h * HALF + i * width, h * HALF + (i + 1) * width)
-                nc.vector.quantize_mx(
-                    out=z_codes[:, piece].bitcast(FP8X4),
-                    scales=z_scales[:, piece],
-                    in_=z[:, i * width * PACK : (i + 1) * width * PACK],
-                )
+            for i in range(2):
+                piece = slice(h * HALF + i * QUARTER, h * HALF + (i + 1) * QUARTER)
+                nc.vector.quantize_mx(out=z_codes[:, piece].bitcast(FP8X4), scales=z_scales[:, piece], in_=z[:, i, :])
 
-        banks = {}
+        for token_half in range(2):
+            project(0, [token_half])
+            project(1, [token_half])
+        b_words = placed.tile([P, S], U32, name="b_words", align_bytes=64, offset=AT_B_WORDS)
+        for h in range(2):
+            for t in range(TILES):
+                fetch_on_scalar(pa[h][:, t, :], y[t], l_n1, cols(h))
+                if h == 0:
+                    nc.vector.tensor_copy(y_bf[:, t, :], y[t][:])
+                    if t == 0:
+                        pick_dealt_words(b_words, l_cb)
+                    if t == 1:
+                        project(2, [0, 1])
+                        project(3, [0, 1])
+                if h == 0:
+                    fetch_on_vector(pb[h][:, t, :], y[t], l_n2, cols(h))
+                else:
+                    fetch_on_scalar(pb[h][:, t, :], y[t], l_n2, cols(h))
+                if t % 2 == 1:
+                    order_pair(h, t // 2)
+            quantize_z(h)
 
-        def score(name, dst, words, scales, t, halves, evacuate):
-            if (name, t) not in banks:
-                banks[name, t] = bank(S, "early" if t >= KEPT and halves == [0] else name)
-            acc = banks[name, t]
-            span = slice(halves[0] * HALF, (halves[-1] + 1) * HALF)
-            product(acc[:, span], words, scales, t, z_codes[:, span], z_scales[:, span])
-            nc.scalar.activation(dst[t][:, evacuate], acc[:, evacuate], COPY, scale=SCORE_SCALE)
-
-        median_half(0)
-        median_half(1)
-        q_picked = placed.tile([P, S], U8, name="q_picked", align_bytes=64, offset=12288 + 1024)
-        q_words = placed.tile([P, S], U32, name="q_words", align_bytes=64, offset=12288 + 1536)
+        q_picked = placed.tile([P, S], U8, name="q_picked", align_bytes=64, offset=AT_Q_PICKED)
+        q_words = placed.tile([P, S], U32, name="q_words", align_bytes=64, offset=AT_Q_WORDS)
         pick_scales(q_picked, l_cd)
         pick_dealt_words(q_words, l_cd)
         q_scales = deal_scales(q_picked, "q_scales")
+        out_rows = out.rearrange("(g t v) c -> t g v c", t=TILES, v=RUN)
+
+        def score(dst, acc, words, scales, t, span):
+            product(acc[:], words, scales, t, z_codes[:, span], z_scales[:, span])
+            nc.scalar.activation(dst[t][:, span], acc[:], COPY, scale=SCORE_SCALE)
+
+        def ring_bank():
+            return psum.tile([P, HALF], F32, name="acc", bufs=7)
+
+        def linked_bank(width):
+            return psum.tile([P, width], F32, name="linked")
+
         for t in range(TILES):
-            score("a", a, a_words, a_scales, t, [0], cols(0))
-            score("b", b, b_words, b_scales, t, [0], cols(0))
-            if t >= KEPT:
-                banks.pop(("a", t))
-                banks.pop(("b", t))
+            score(a, ring_bank(), a_words, a_scales, t, cols(0))
+            score(b, ring_bank(), b_words, b_scales, t, cols(0))
 
-        out_rows = out.rearrange("(a t v) c -> t a v c", t=TILES, v=4)
-        m1 = {}
-        m6 = {}
-        upper = [keep.tile([P, S], F32, name=f"upper{t}") for t in range(TILES)]
-        whole = [slice(0, S)]
-        halves = [cols(0), cols(1)]
+        m1, m6, q7, upper, lower = {}, {}, {}, {}, {}
 
-        def fetch_row(dst, window, lst, vector_halves):
-            if len(vector_halves) == 1:
-                for h in range(2):
-                    fetch(dst[:, cols(h)], window, half_of(lst, h), h in vector_halves)
-            else:
-                fetch(dst[:], window, lst[:], len(vector_halves) == 2)
+        def fetch_m6(t, pieces):
+            m6[t] = work.tile([P, S], F32, name="m6")
+            for piece in pieces:
+                fetch_on_scalar(m6[t][:, piece], m1[t], l_n6, piece)
 
-        def second_scores(t):
-            score("a", a, a_words, a_scales, t, [1] if t < KEPT else [0, 1], cols(1))
-            score("b", b, b_words, b_scales, t, [1] if t < KEPT else [0, 1], cols(1))
+        def make_upper(t):
+            upper[t] = work.tile([P, S], F32, name="upper")
+            nc.vector.tensor_tensor(upper[t][:], m1[t][:, whole], q7[t][:], ALU.max)
 
-        q7 = {}
-        last = TILES - 1
+        def make_lower(t, pieces, tag):
+            lower[t] = work.tile([P, S], F32, name="lower", tag=tag, bufs=1)
+            for piece in pieces:
+                nc.vector.tensor_tensor(lower[t][:, piece], m6[t][:, piece], q[t][:, piece], ALU.min)
 
-        def fetch_shared(dst, window, lst, share, scale=1.0):
-            split = S - share
-            if split > 0:
-                nc.scalar.activation(dst[:, :split], window[:].indirect(lst[:, : split // 16]), COPY, scale=scale)
-            if split < S:
-                fetch(dst[:, split:], window, lst[:, split // 16 :], True)
+        def store(t, pieces):
+            res = work.tile([P, S], F32, name="res")
+            for piece in pieces:
+                nc.vector.tensor_tensor(res[:, piece], upper[t][:, piece], lower[t][:, piece], ALU.subtract)
+                nc.sync.dma_start(out_rows[t][:, :, piece], res[:, piece])
 
-        def flow(t):
-            a3 = work.tile([P, S], F32, name="a3")
-            a4 = work.tile([P, S], F32, name="a4")
-            b5 = work.tile([P, S], F32, name="b5")
+        def step(t):
+            a3 = work.tile([P, S], F32, name="a3", bufs=1)
+            a4 = work.tile([P, S], F32, name="a4", bufs=1)
             d3 = work.tile([P, S], F32, name="d3")
             d4 = work.tile([P, S], F32, name="d4")
             e3 = work.tile([P, S], F32, name="e3")
-            e4 = work.tile([P, S], F32, name="e4")
-            m1[t] = keep.tile([P, 2 * S], F32, name=f"m1_{t}")
-            fetch_shared(a4, a[t], l_n4, 0, 0.5)
-            fetch_shared(a3, a[t], l_n3, SHARE_A3[t])
-            fetch_shared(b5, b[t], l_n5, SHARE_B5[t])
-            nc.vector.scalar_tensor_tensor(d4[:], banks["a", t][:], -0.5 * SCORE_SCALE, a4[:], ALU.mult, ALU.add)
-            (nc.gpsimd if t in POOL_E4 else nc.vector).tensor_tensor(e4[:], b5[:], d4[:], ALU.mult)
-            pieces = halves if t == last else whole
-            for piece in pieces:
-                nc.vector.scalar_tensor_tensor(
-                    d3[:, piece], banks["a", t][:, piece], -SCORE_SCALE, a3[:, piece], ALU.mult, ALU.add
-                )
-            for piece in pieces:
-                nc.vector.scalar_tensor_tensor(
-                    e3[:, piece], banks["b", t][:, piece], SCORE_SCALE, d3[:, piece], ALU.mult, ALU.mult
-                )
-            for piece in pieces:
-                engine = nc.gpsimd if t in POOL_M1 else nc.vector
-                engine.tensor_tensor(m1[t][:, piece], e4[:, piece], e3[:, piece], ALU.add)
-
-        def fetch_q7(t):
-            score("q", q, q_words, q_scales, t, [0, 1], slice(0, S))
-            q7[t] = work.tile([P, S], F32, name="q7")
-            fetch(q7[t][:], q[t], l_n7[:], False)
-
-        def fetch_m6(t):
-            m6[t] = work.tile([P, S], F32, name="m6")
-            if t == last:
-                for h in range(2):
-                    fetch(m6[t][:, cols(h)], m1[t], half_of(l_n6, h), False)
+            e4 = work.tile([P, S], F32, name="e4", bufs=1)
+            fetch_on_scalar(a4[:], a[t], l_n4, whole)
+            if t < SHARED:
+                fetch_on_scalar(a3[:, cols(0)], a[t], l_n3, cols(0))
+                fetch_on_vector(a3[:, cols(1)], a[t], l_n3, cols(1))
             else:
-                fetch(m6[t][:], m1[t], l_n6[:], False)
-
-        def finish(t, pieces, engine):
-            lower = work.tile([P, S], F32, name="lower")
-            res = work.tile([P, S], F32, name="res")
-            nc.vector.tensor_tensor(upper[t][:], m1[t][:, :S], q7[t][:], ALU.max)
+                fetch_on_scalar(a3[:], a[t], l_n3, whole)
+            score(q, linked_bank(S), q_words, q_scales, t, whole)
+            if t > 0:
+                fetch_m6(t - 1, [whole])
+            if t < LAST:
+                score(b, ring_bank(), b_words, b_scales, t + 1, cols(1))
+                score(a, linked_bank(HALF), a_words, a_scales, t + 1, cols(1))
+            nc.vector.tensor_tensor(d4[:], a4[:], a[t][:, whole], ALU.subtract)
+            if t > 0:
+                make_upper(t - 1)
+            q7[t] = keep.tile([P, S], F32, name="q7", tag=f"chain{t}")
+            fetch_on_scalar(q7[t][:], q[t], l_n7, whole)
+            nc.vector.tensor_tensor(e4[:], b[t][:].indirect(l_n5[:]), d4[:], ALU.mult)
+            pieces = halves if t in (0, LAST) else [whole]
             for piece in pieces:
-                nc.vector.scalar_tensor_tensor(
-                    lower[:, piece], banks["q", t][:, piece], SCORE_SCALE, m6[t][:, piece], ALU.mult, ALU.min
-                )
+                nc.vector.tensor_tensor(d3[:, piece], a3[:, piece], a[t][:, piece], ALU.subtract)
+            if 0 < t < LAST:
+                make_lower(t - 1, [whole], "lower")
             for piece in pieces:
-                engine.tensor_tensor(res[:, piece], upper[t][:, piece], lower[:, piece], ALU.subtract)
-                nc.sync.dma_start(out_rows[t][:, :, piece], res[:, piece])
+                nc.vector.tensor_tensor(e3[:, piece], d3[:, piece], b[t][:, piece], ALU.mult)
+            if 0 < t < LAST:
+                store(t - 1, [whole])
+            m1[t] = keep.tile([P, 2 * S], F32, name=f"m1_{t}", tag=f"chain{t + 1}")
+            for piece in pieces:
+                nc.vector.scalar_tensor_tensor(m1[t][:, piece], e4[:, piece], 0.5, e3[:, piece], ALU.mult, ALU.add)
 
-        second_scores(0)
-        second_scores(1)
+        score(a, linked_bank(HALF), a_words, a_scales, 0, cols(1))
+        score(b, ring_bank(), b_words, b_scales, 0, cols(1))
         for t in range(TILES):
-            flow(t)
-            if t > 0:
-                fetch_m6(t - 1)
-            fetch_q7(t)
-            if t + 2 < TILES:
-                second_scores(t + 2)
-            if t > 0:
-                finish(t - 1, whole, nc.gpsimd if t - 1 in POOL_RES else nc.vector)
-        fetch_m6(last)
-        finish(last, halves, nc.vector)
+            step(t)
+
+        fetch_m6(LAST, halves)
+        make_lower(LAST - 1, [whole], "e4")
+        make_upper(LAST)
+        store(LAST - 1, [whole])
+        make_lower(LAST, halves, "lower")
+        store(LAST, halves)

@@ -24,15 +24,15 @@ QUARTER = S // 4
 STRIPE = 16
 RUN = 4
 SCORE_SCALE = 0.0625
-SHARED = 2
+RING_BANKS = 7
 
 AT_W_BF = (2048, 6144)
 AT_A_WORDS = 512
 AT_TOKEN_WORDS = (2560, 3584)
 AT_B_WORDS = 5120
-AT_Z = (8192, 12288)
-AT_Q_PICKED = 12288
-AT_Q_WORDS = 13312
+AT_Z = ((8192, 9216), (11264, 14336))
+AT_Q_PICKED = 11264
+AT_Q_WORDS = 11776
 
 
 def tile_picked_tricdflowbmaxbmed_none_p_kernel(
@@ -163,7 +163,7 @@ def tile_picked_tricdflowbmaxbmed_none_p_kernel(
         y_bf = keep.tile([P, TILES, S], BF16, name="y_bf")
 
         def project(t, token_halves):
-            acc = psum.tile([P, HALF * len(token_halves)], F32, name="acc", bufs=7)
+            acc = psum.tile([P, HALF * len(token_halves)], F32, name="acc", bufs=RING_BANKS)
             for i, h in enumerate(token_halves):
                 product(
                     acc[:, cols(i)], w_codes[t // 2], w_scales[t // 2], t % 2, token_words[h][:], token_scales[:, cols(h)]
@@ -185,17 +185,20 @@ def tile_picked_tricdflowbmaxbmed_none_p_kernel(
                 nc.vector.tensor_tensor(mid[h][:, ts, piece], high[h][:, ts, piece], pb[h][:, ts, piece], ALU.min)
 
         def quantize_z(h):
-            z = placed.tile([P, 2, QUARTER * PACK], BF16, name=f"z{h}", align_bytes=64, offset=AT_Z[h])
+            z = [
+                placed.tile([P, QUARTER * PACK], BF16, name=f"z{h}_{i}", align_bytes=64, offset=AT_Z[h][i])
+                for i in range(2)
+            ]
             for i, piece in enumerate(quarters):
                 nc.vector.tensor_tensor(
-                    z[:, i, :].rearrange("p (c n t) -> p c t n", n=4, t=PACK),
+                    z[i][:].rearrange("p (c n t) -> p c t n", n=4, t=PACK),
                     low[h][:, :, piece].rearrange("p t (c n) -> p c t n", n=4),
                     mid[h][:, :, piece].rearrange("p t (c n) -> p c t n", n=4),
                     ALU.max,
                 )
             for i in range(2):
                 piece = slice(h * HALF + i * QUARTER, h * HALF + (i + 1) * QUARTER)
-                nc.vector.quantize_mx(out=z_codes[:, piece].bitcast(FP8X4), scales=z_scales[:, piece], in_=z[:, i, :])
+                nc.vector.quantize_mx(out=z_codes[:, piece].bitcast(FP8X4), scales=z_scales[:, piece], in_=z[i][:])
 
         for token_half in range(2):
             project(0, [token_half])
@@ -231,7 +234,7 @@ def tile_picked_tricdflowbmaxbmed_none_p_kernel(
             nc.scalar.activation(dst[t][:, span], acc[:], COPY, scale=SCORE_SCALE)
 
         def ring_bank():
-            return psum.tile([P, HALF], F32, name="acc", bufs=7)
+            return psum.tile([P, HALF], F32, name="acc", bufs=RING_BANKS)
 
         def linked_bank(width):
             return psum.tile([P, width], F32, name="linked")
@@ -265,16 +268,18 @@ def tile_picked_tricdflowbmaxbmed_none_p_kernel(
         def step(t):
             a3 = work.tile([P, S], F32, name="a3", bufs=1)
             a4 = work.tile([P, S], F32, name="a4", bufs=1)
-            d3 = work.tile([P, S], F32, name="d3")
+            d3 = work.tile([P, S], F32, name="d3", bufs=1)
             d4 = work.tile([P, S], F32, name="d4")
             e3 = work.tile([P, S], F32, name="e3")
             e4 = work.tile([P, S], F32, name="e4", bufs=1)
             fetch_on_scalar(a4[:], a[t], l_n4, whole)
-            if t < SHARED:
+            if t == LAST:
+                b5 = work.tile([P, HALF], F32, name="b5")
+                fetch_on_scalar(b5[:], b[t], l_n5, cols(1))
+                fetch_on_scalar(a3[:], a[t], l_n3, whole)
+            else:
                 fetch_on_scalar(a3[:, cols(0)], a[t], l_n3, cols(0))
                 fetch_on_vector(a3[:, cols(1)], a[t], l_n3, cols(1))
-            else:
-                fetch_on_scalar(a3[:], a[t], l_n3, whole)
             score(q, linked_bank(S), q_words, q_scales, t, whole)
             if t > 0:
                 fetch_m6(t - 1, [whole])
@@ -286,10 +291,16 @@ def tile_picked_tricdflowbmaxbmed_none_p_kernel(
                 make_upper(t - 1)
             q7[t] = keep.tile([P, S], F32, name="q7", tag=f"chain{t}")
             fetch_on_scalar(q7[t][:], q[t], l_n7, whole)
-            nc.vector.tensor_tensor(e4[:], b[t][:].indirect(l_n5[:]), d4[:], ALU.mult)
+            if t == 0:
+                nc.vector.tensor_tensor(d3[:], a3[:], a[t][:, whole], ALU.subtract)
+            fused = cols(0) if t == LAST else whole
+            nc.vector.tensor_tensor(e4[:, fused], b[t][:].indirect(entries(l_n5, fused)), d4[:, fused], ALU.mult)
+            if t == LAST:
+                nc.vector.tensor_tensor(e4[:, cols(1)], b5[:], d4[:, cols(1)], ALU.mult)
             pieces = halves if t in (0, LAST) else [whole]
-            for piece in pieces:
-                nc.vector.tensor_tensor(d3[:, piece], a3[:, piece], a[t][:, piece], ALU.subtract)
+            if t > 0:
+                for piece in pieces:
+                    nc.vector.tensor_tensor(d3[:, piece], a3[:, piece], a[t][:, piece], ALU.subtract)
             if 0 < t < LAST:
                 make_lower(t - 1, [whole], "lower")
             for piece in pieces:
@@ -306,7 +317,7 @@ def tile_picked_tricdflowbmaxbmed_none_p_kernel(
             step(t)
 
         fetch_m6(LAST, halves)
-        make_lower(LAST - 1, [whole], "e4")
+        make_lower(LAST - 1, [whole], "d3")
         make_upper(LAST)
         store(LAST - 1, [whole])
         make_lower(LAST, halves, "lower")

from contextlib import ExitStack

import concourse.mybir as mybir

T, S, H = 2048, 512, 512
FLOPS = 4 * 2 * 512 * 512 * 512

F32 = mybir.dt.float32
BF16 = mybir.dt.bfloat16
I32 = mybir.dt.int32
U32 = mybir.dt.uint32
U16 = mybir.dt.uint16
U8 = mybir.dt.uint8
FP8X4 = mybir.dt.float8_e4m3fn_x4
ALU = mybir.AluOpType
COPY = mybir.ActivationFunctionType.Copy

P = 128
PACK = 4
TILES = 4
LAST = TILES - 1
HALF = S // 2
QUARTER = S // 4
STRIPE = 16
RUN = 4
SCORE_SCALE = 0.0625
RING_BANKS = 7

AT_W_BF = (2048, 6144)
AT_A_WORDS = 512
AT_TOKEN_WORDS = (2560, 3584)
AT_B_WORDS = 5120
AT_Z = ((8192, 9216), (11264, 14336))
AT_Q_PICKED = 11264
AT_Q_WORDS = 11776


def tile_picked_tricdflowbmaxbmed_none_p_kernel(
    tc, x_words, x_scales, w1, gs, offs, n1, n2, ca, cb, cd, n3, n4, n5, n6, n7, out
):
    nc = tc.nc
    with ExitStack() as ctx:
        lists = ctx.enter_context(tc.tile_pool(name="lists", bufs=1))
        keep = ctx.enter_context(tc.tile_pool(name="keep", bufs=1))
        placed = ctx.enter_context(tc.tile_pool(name="placed", bufs=1))
        work = ctx.enter_context(tc.tile_pool(name="work", bufs=2))
        psum = ctx.enter_context(tc.psum_pool(name="psum", bufs=1))

        def load_list(src, name):
            dst = lists.tile([P, S // STRIPE], U16, name=name)
            nc.sync.dma_start(dst[:], src)
            return dst

        def cols(h):
            return slice(h * HALF, (h + 1) * HALF)

        def entries(lst, span):
            return lst[:, span.start // STRIPE : span.stop // STRIPE]

        whole = slice(0, S)
        halves = [cols(0), cols(1)]

        l_offs = load_list(offs, "l_offs")
        l_ca = load_list(ca, "l_ca")
        l_cb = load_list(cb, "l_cb")
        table_scales = keep.tile([P, T], U8, name="table_scales", align_bytes=64)
        nc.vector.memset(table_scales[:].bitcast(I32), 0)
        for quad in range(4):
            nc.sync.dma_start(
                table_scales[32 * quad : 32 * quad + 4, :].bitcast(I32),
                x_scales[0, 4 * quad : 4 * quad + 4, :].bitcast(I32),
            )
        w_raw = keep.tile([P, PACK, H], F32, name="w_raw")
        nc.sync.dma_start(w_raw[:], w1.rearrange("(p j) c -> p j c", j=PACK))
        table_words = keep.tile([P, T], U32, name="table_words", align_bytes=64)
        nc.sync.dma_start(table_words[:].bitcast(I32), x_words[0].rearrange("p n r -> p (n r)").bitcast(I32))
        gain = keep.tile([P, TILES], F32, name="gain")
        nc.sync.dma_start(gain[:], gs.rearrange("(p t) o -> p (t o)", t=TILES))
        l_n1 = load_list(n1, "l_n1")
        l_n2 = load_list(n2, "l_n2")
        l_cd = load_list(cd, "l_cd")
        l_n3 = load_list(n3, "l_n3")
        l_n4 = load_list(n4, "l_n4")
        l_n5 = load_list(n5, "l_n5")
        l_n7 = load_list(n7, "l_n7")
        l_n6 = load_list(n6, "l_n6")

        def pick_scales(dst, lst):
            nc.vector.tensor_copy(dst[:], table_scales[:].indirect(lst[:]))

        def deal_scales(picked, name):
            dst = keep.tile([P, S], U8, name=name, align_bytes=64)
            nc.vector.tensor_copy(
                dst[:].bitcast(I32).rearrange("p (t g) -> p t g", t=TILES),
                picked[:].bitcast(I32).rearrange("p (g t) -> p t g", t=TILES),
            )
            return dst

        def pick_dealt_words(dst, lst):
            nc.vector.tensor_copy(
                dst[:].rearrange("p (t g v) -> p g t v", t=TILES, v=RUN), table_words[:].indirect(lst[:])
            )

        token_scales = keep.tile([P, S], U8, name="token_scales", align_bytes=64)
        a_picked = keep.tile([P, S], U8, name="a_picked", align_bytes=64)
        b_picked = keep.tile([P, S], U8, name="b_picked", align_bytes=64)
        pick_scales(token_scales, l_offs)
        pick_scales(a_picked, l_ca)
        pick_scales(b_picked, l_cb)
        a_scales = deal_scales(a_picked, "a_scales")
        b_scales = deal_scales(b_picked, "b_scales")

        w_codes = [keep.tile([P, HALF], U32, name=f"w_codes{pair}", align_bytes=64) for pair in range(2)]
        w_scales = [keep.tile([P, HALF], U8, name=f"w_scales{pair}", align_bytes=64) for pair in range(2)]

        def quantize_weights(pair):
            w_bf = placed.tile([P, 2, P, PACK], BF16, name=f"w_bf{pair}", align_bytes=64, offset=AT_W_BF[pair])
            nc.scalar.copy(
                w_bf[:].rearrange("p t m j -> p m j t"),
                w_raw[:].rearrange("p j (m t) -> p m j t", t=TILES)[:, :, :, 2 * pair : 2 * pair + 2],
            )
            nc.vector.quantize_mx(
                out=w_codes[pair][:].bitcast(FP8X4),
                scales=w_scales[pair][:],
                in_=w_bf[:].rearrange("p t m j -> p (t m j)"),
            )

        quantize_weights(0)
        token_words = [
            placed.tile([P, HALF], U32, name=f"token_words{h}", align_bytes=64, offset=AT_TOKEN_WORDS[h])
            for h in range(2)
        ]
        for h in range(2):
            nc.vector.tensor_copy(token_words[h][:], table_words[:].indirect(entries(l_offs, cols(h))))
        quantize_weights(1)
        a_words = placed.tile([P, S], U32, name="a_words", align_bytes=64, offset=AT_A_WORDS)
        pick_dealt_words(a_words, l_ca)

        def product(acc, lhs_words, lhs_scales, block, rhs_words, rhs_scales):
            rows = slice(block * P, (block + 1) * P)
            nc.tensor.matmul_mx(
                out=acc,
                lhsT=lhs_words[:, rows].bitcast(FP8X4),
                lhsT_scale=lhs_scales[:, rows],
                rhs=rhs_words.bitcast(FP8X4),
                rhs_scale=rhs_scales,
                start=True,
                stop=True,
            )

        def fetch_on_scalar(dst, window, lst, span):
            nc.scalar.activation(dst, window[:].indirect(entries(lst, span)), COPY)

        def fetch_on_vector(dst, window, lst, span):
            nc.vector.tensor_copy(dst, window[:].indirect(entries(lst, span)))

        y = [keep.tile([P, S], F32, name=f"y{t}") for t in range(TILES)]
        a = [keep.tile([P, 2 * S], F32, name=f"a{t}") for t in range(TILES)]
        b = [keep.tile([P, 2 * S], F32, name=f"b{t}") for t in range(TILES)]
        q = [keep.tile([P, 2 * S], F32, name=f"q{t}") for t in range(TILES)]
        z_codes = keep.tile([P, S], U32, name="z_codes", align_bytes=64)
        z_scales = keep.tile([P, S], U8, name="z_scales", align_bytes=64)
        y_bf = keep.tile([P, TILES, S], BF16, name="y_bf")

        def project(t, token_halves):
            acc = psum.tile([P, HALF * len(token_halves)], F32, name="acc", bufs=RING_BANKS)
            for i, h in enumerate(token_halves):
                product(
                    acc[:, cols(i)], w_codes[t // 2], w_scales[t // 2], t % 2, token_words[h][:], token_scales[:, cols(h)]
                )
            span = slice(token_halves[0] * HALF, (token_halves[-1] + 1) * HALF)
            nc.scalar.activation(y[t][:, span], acc[:], COPY, scale=gain[:, t : t + 1])

        low, mid, pa, pb, high = (
            [work.tile([P, TILES, HALF], BF16, name=name) for h in range(2)]
            for name in ("low", "mid", "pa", "pb", "high")
        )
        quarters = [slice(i * QUARTER, (i + 1) * QUARTER) for i in range(2)]

        def order_pair(h, pair):
            ts = slice(2 * pair, 2 * pair + 2)
            nc.vector.tensor_tensor(high[h][:, ts, :], y_bf[:, ts, cols(h)], pa[h][:, ts, :], ALU.max)
            nc.vector.tensor_tensor(low[h][:, ts, :], y_bf[:, ts, cols(h)], pa[h][:, ts, :], ALU.min)
            for piece in quarters if pair == 1 else [slice(0, HALF)]:
                nc.vector.tensor_tensor(mid[h][:, ts, piece], high[h][:, ts, piece], pb[h][:, ts, piece], ALU.min)

        def quantize_z(h):
            z = [
                placed.tile([P, QUARTER * PACK], BF16, name=f"z{h}_{i}", align_bytes=64, offset=AT_Z[h][i])
                for i in range(2)
            ]
            for i, piece in enumerate(quarters):
                nc.vector.tensor_tensor(
                    z[i][:].rearrange("p (c n t) -> p c t n", n=4, t=PACK),
                    low[h][:, :, piece].rearrange("p t (c n) -> p c t n", n=4),
                    mid[h][:, :, piece].rearrange("p t (c n) -> p c t n", n=4),
                    ALU.max,
                )
            for i in range(2):
                piece = slice(h * HALF + i * QUARTER, h * HALF + (i + 1) * QUARTER)
                nc.vector.quantize_mx(out=z_codes[:, piece].bitcast(FP8X4), scales=z_scales[:, piece], in_=z[i][:])

        for token_half in range(2):
            project(0, [token_half])
            project(1, [token_half])
        b_words = placed.tile([P, S], U32, name="b_words", align_bytes=64, offset=AT_B_WORDS)
        for h in range(2):
            for t in range(TILES):
                fetch_on_scalar(pa[h][:, t, :], y[t], l_n1, cols(h))
                if h == 0:
                    nc.vector.tensor_copy(y_bf[:, t, :], y[t][:])
                    if t == 0:
                        pick_dealt_words(b_words, l_cb)
                    if t == 1:
                        project(2, [0, 1])
                        project(3, [0, 1])
                if h == 0:
                    fetch_on_vector(pb[h][:, t, :], y[t], l_n2, cols(h))
                else:
                    fetch_on_scalar(pb[h][:, t, :], y[t], l_n2, cols(h))
                if t % 2 == 1:
                    order_pair(h, t // 2)
            quantize_z(h)

        q_picked = placed.tile([P, S], U8, name="q_picked", align_bytes=64, offset=AT_Q_PICKED)
        q_words = placed.tile([P, S], U32, name="q_words", align_bytes=64, offset=AT_Q_WORDS)
        pick_scales(q_picked, l_cd)
        pick_dealt_words(q_words, l_cd)
        q_scales = deal_scales(q_picked, "q_scales")
        out_rows = out.rearrange("(g t v) c -> t g v c", t=TILES, v=RUN)

        def score(dst, acc, words, scales, t, span):
            product(acc[:], words, scales, t, z_codes[:, span], z_scales[:, span])
            nc.scalar.activation(dst[t][:, span], acc[:], COPY, scale=SCORE_SCALE)

        def ring_bank():
            return psum.tile([P, HALF], F32, name="acc", bufs=RING_BANKS)

        def linked_bank(width):
            return psum.tile([P, width], F32, name="linked")

        for t in range(TILES):
            score(a, ring_bank(), a_words, a_scales, t, cols(0))
            score(b, ring_bank(), b_words, b_scales, t, cols(0))

        m1, m6, q7, upper, lower = {}, {}, {}, {}, {}

        def fetch_m6(t, pieces):
            m6[t] = work.tile([P, S], F32, name="m6")
            for piece in pieces:
                fetch_on_scalar(m6[t][:, piece], m1[t], l_n6, piece)

        def make_upper(t):
            upper[t] = work.tile([P, S], F32, name="upper")
            nc.vector.tensor_tensor(upper[t][:], m1[t][:, whole], q7[t][:], ALU.max)

        def make_lower(t, pieces, tag):
            lower[t] = work.tile([P, S], F32, name="lower", tag=tag, bufs=1)
            for piece in pieces:
                nc.vector.tensor_tensor(lower[t][:, piece], m6[t][:, piece], q[t][:, piece], ALU.min)

        def store(t, pieces):
            res = work.tile([P, S], F32, name="res")
            for piece in pieces:
                nc.vector.tensor_tensor(res[:, piece], upper[t][:, piece], lower[t][:, piece], ALU.subtract)
                nc.sync.dma_start(out_rows[t][:, :, piece], res[:, piece])

        def step(t):
            a3 = work.tile([P, S], F32, name="a3", bufs=1)
            a4 = work.tile([P, S], F32, name="a4", bufs=1)
            d3 = work.tile([P, S], F32, name="d3", bufs=1)
            d4 = work.tile([P, S], F32, name="d4")
            e3 = work.tile([P, S], F32, name="e3")
            e4 = work.tile([P, S], F32, name="e4", bufs=1)
            fetch_on_scalar(a4[:], a[t], l_n4, whole)
            if t == LAST:
                b5 = work.tile([P, HALF], F32, name="b5")
                fetch_on_scalar(b5[:], b[t], l_n5, cols(1))
                fetch_on_scalar(a3[:], a[t], l_n3, whole)
            else:
                fetch_on_scalar(a3[:, cols(0)], a[t], l_n3, cols(0))
                fetch_on_vector(a3[:, cols(1)], a[t], l_n3, cols(1))
            score(q, linked_bank(S), q_words, q_scales, t, whole)
            if t > 0:
                fetch_m6(t - 1, [whole])
            if t < LAST:
                score(b, ring_bank(), b_words, b_scales, t + 1, cols(1))
                score(a, linked_bank(HALF), a_words, a_scales, t + 1, cols(1))
            nc.vector.tensor_tensor(d4[:], a4[:], a[t][:, whole], ALU.subtract)
            if t > 0:
                make_upper(t - 1)
            q7[t] = keep.tile([P, S], F32, name="q7", tag=f"chain{t}")
            fetch_on_scalar(q7[t][:], q[t], l_n7, whole)
            if t == 0:
                nc.vector.tensor_tensor(d3[:], a3[:], a[t][:, whole], ALU.subtract)
            fused = cols(0) if t == LAST else whole
            nc.vector.tensor_tensor(e4[:, fused], b[t][:].indirect(entries(l_n5, fused)), d4[:, fused], ALU.mult)
            if t == LAST:
                nc.vector.tensor_tensor(e4[:, cols(1)], b5[:], d4[:, cols(1)], ALU.mult)
            pieces = halves if t in (0, LAST) else [whole]
            if t > 0:
                for piece in pieces:
                    nc.vector.tensor_tensor(d3[:, piece], a3[:, piece], a[t][:, piece], ALU.subtract)
            if 0 < t < LAST:
                make_lower(t - 1, [whole], "lower")
            for piece in pieces:
                nc.vector.tensor_tensor(e3[:, piece], d3[:, piece], b[t][:, piece], ALU.mult)
            if 0 < t < LAST:
                store(t - 1, [whole])
            m1[t] = keep.tile([P, 2 * S], F32, name=f"m1_{t}", tag=f"chain{t + 1}")
            for piece in pieces:
                nc.vector.scalar_tensor_tensor(m1[t][:, piece], e4[:, piece], 0.5, e3[:, piece], ALU.mult, ALU.add)

        score(a, linked_bank(HALF), a_words, a_scales, 0, cols(1))
        score(b, ring_bank(), b_words, b_scales, 0, cols(1))
        for t in range(TILES):
            step(t)

        fetch_m6(LAST, halves)
        make_lower(LAST - 1, [whole], "d3")
        make_upper(LAST)
        store(LAST - 1, [whole])
        make_lower(LAST, halves, "lower")
        store(LAST, halves)
